import numpy as np, ml_dtypes
CORES = [2,3,42,43,82,83,122,123]
N = 8
BF = ml_dtypes.bfloat16
V, H, M, CAP, R = 2048, 128, 1, 32, 3
L = M * H
def lanes(t, r):
    c = (M * (N * t + r) + np.arange(M)) & 15
    return (16 * np.arange(H)[None, :] + c[:, None]).reshape(-1)
def pack(b, x, lm):
    return {"nb": np.ascontiguousarray(b.reshape(N, 128, V)).astype(np.float32), "xs": np.ascontiguousarray(x.reshape(N, 128, V)).astype(np.float32).astype(BF),
            "lim": np.ascontiguousarray(lm.reshape(N, 128, 1)).astype(np.int32)}
def parts(rng):
    dens = rng.choice(np.array([0.08, 0.25, 0.5, 0.8]), (N, 8, 1, V)); u = rng.random((N, 8, 16, V))
    h = np.minimum((V * u * u).astype(np.int64), V - 1)
    pool = rng.integers(V // 4, V, (8, 12)); known = pool[np.arange(8)[None, :, None, None], rng.integers(0, 12, (N, 8, 16, V))]
    h = np.where(rng.random((N, 8, 16, V)) < 0.35, known, h)
    b = np.where(rng.random((N, 8, 16, V)) < dens, h, V)
    top = np.where(rng.random((N, 8, 1, V)) < 0.02, 256, rng.choice(np.array([4, 16, 40, 64]), (N, 8, 1, V)))
    x = (top * rng.random((N, 8, 16, V))).astype(np.int64)
    lm = rng.permutation(np.array([6, 16, 28, 45, 70, 110, 180, 300]))[None, :, None] + rng.integers(0, 8, (N, 8, 16))
    return b, x, lm
def late(rng, b, x, lm, g):
    E = np.stack([np.append(rng.permutation(lanes(0, r)[:-1]), lanes(0, r)[-1])[-26:] for r in range(N)])
    C = np.stack([np.append(rng.permutation(lanes(1, r)[:-1]), lanes(1, r)[-1])[-14:] for r in range(N)])
    D = np.stack([rng.permutation(np.setdiff1d(lanes(2, r), E[r]))[:4] for r in range(N)])
    low = E[:, :12]; own = E[:, 12:18]; top = E[:, 18:]; lows = low.reshape(-1)
    pool = np.setdiff1d(np.arange(V), np.concatenate([E.reshape(-1), C.reshape(-1), D.reshape(-1)]))
    b[:, g] = rng.choice(pool, (N, 16, V)); x[:, g] = rng.integers(128, 256, (N, 16, V)); lm[:, g] = rng.integers(600, 1600, (N, 16))
    for r in range(N):
        b[r, g][:, E[r]] = V; b[r, g][:, C[r, :3]] = V
    for r in range(N):
        z = rng.permutation(pool)[:12]; x[r, g][:, z] = 255; x[r, g][rng.integers(0, 16, 12), z] = 254
        b[r, g][rng.integers(0, 16, 12), low[r]] = z
        p = rng.integers(0, 16, 8); b[r, g][p, top[r]] = rng.choice(pool, 8); b[r, g][(p + rng.integers(1, 16, 8)) & 15, top[r]] = rng.choice(pool, 8)
        q = (r + 1) % N; s = C[r, :6]; k = rng.integers(0, 16, 6); j = (k + rng.integers(1, 16, 6)) & 15
        b[q, g][k, own[q]] = s; b[r, g][k, s] = s; b[r, g][j, s] = own[q]
        for i in range(8):
            n = rng.permutation(lows)[:16]; n[12 + (i & 3)] = top[q, i] if i < 4 else top[0, i]
            b[r, g][:, C[r, 6 + i]] = n
        if r < N - 1:
            for i in range(4):
                n = rng.permutation(lows)[:16]; n[int(rng.integers(0, 16))] = top[0, 4 + i]
                b[r, g][:, D[r, i]] = n
def setup_inputs(rng):
    return pack(*parts(rng))
def setup_inputs_spread(rng):
    d = rng.random((N, 8, 1, V))
    b = np.where(rng.random((N, 8, 16, V)) < d * d * d, rng.integers(0, V, (N, 8, 16, V)), V)
    x = np.minimum((np.exp2(8 * rng.random((N, 8, 1, V))) * rng.random((N, 8, 16, V))).astype(np.int64), 255)
    lm = np.minimum((np.exp2(3 + 9 * rng.random((N, 8, 1))) * (0.5 + 0.5 * rng.random((N, 8, 16)))).astype(np.int64), 4079)
    return pack(b, x, lm)
def setup_inputs_ends(rng):
    x = 255 * np.where(rng.random((N, 8, 1, V)) < 0.5, rng.integers(0, 2, (N, 8, 1, V)), rng.integers(0, 2, (N, 8, 16, V)))
    x[:, 1::2, :, :16] = 255; x[:, 1::2, :, V - 1] = 255
    mode = rng.choice(np.array([0, 0, 1, 2, 2, 2, 3, 4]), (N, 8, 1, V)); coin = rng.integers(0, 2, (N, 8, 16, V))
    v = np.arange(V)[None, :]; p = np.arange(16)[:, None]
    b = np.where(mode == 0, 0, np.where(mode == 1, V, np.where(mode == 2, coin * V, np.where(mode == 3, np.where(coin == 1, p, V - 1), rng.integers(0, V + 1, (N, 8, 16, V))))))
    b[:, 0:6:2, :, 0:16:2] = V
    b[:, 3:6:2, :, 0:16] = V; b[:, 3:6:2, 5, 0:16] = 0
    b[N - 1, 7] = np.where((v >= V - 192) & (p == ((v >> 4) & 15)), V, 0)
    big = np.array([9, 16, 8, 16, 0, 9, 12, 16])[None, :, None]
    lm = np.where(np.argsort(rng.random((N, 8, 16)), axis=2) < big, 4079, 0)
    return pack(b, x, lm)
def setup_inputs_corners(rng):
    x = rng.integers(16, 32, (N, 8, 16, V)); x[..., V - 80:V - 16] = 255; x[..., V - 16:] = 0
    pos = np.argsort(rng.random((N, 8, 16, V)), axis=2)
    many = np.where((rng.random((N, 8, 16, V)) < 0.4) | (pos < 4), rng.integers(0, V - 16, (N, 8, 16, V)), V)
    one = np.where(pos == 0, rng.integers(0, V - 80, (N, 8, 16, V)), V)
    kind = rng.choice(np.array([0, 1, 2, 2]), (N, 8, 1, V)); counts = (CAP, CAP + 1, L, CAP - 1, 1, 0, CAP, 2)
    for q in range(N):
        v = lanes(0, q)
        for g in range(8):
            n = counts[(g + 3 * q) % 8]; o = rng.permutation(L)
            kind[q, g, 0, v[o[:n]]] = 0 if g % 4 == 2 else rng.integers(0, 2, n)
            kind[q, g, 0, v[o[n:]]] = rng.integers(1, 3, L - n) if g % 4 == 2 else 2
    b = np.where(kind == 0, V, np.where(kind == 1, one, many))
    lm = 40 + rng.integers(0, 8, (N, 8, 16)); o = np.argsort(rng.random((N, 8, 16)), axis=2)
    lm[:, 1::2] = np.where(o[:, 1::2] < 9, lm[:, 1::2], 0); lm[:, 2::4] = np.where(o[:, 2::4] < 8, lm[:, 2::4], 0)
    return pack(b, x, lm)
def setup_inputs_crowd(rng):
    b, x, lm = parts(rng)
    b[:, :4] = np.where(rng.random((N, 4, 16, V)) < 0.1, rng.integers(V - 128, V, (N, 4, 16, V)), V); b[:, :4, 0, :] = 0
    v = np.arange(V)
    for t in range(16 // (N * M)):
        c = (M * (N * t + N - 1)) & 15
        b[:, 1:4:2, 0, np.flatnonzero(((v & 15) == c) & ((v >> 4) % CAP == CAP - 1))] = V
    lm[:, :4] = 4079; x[:, :2] = 255
    b[:, 4:] = np.where(b[:, 4:] < V, rng.choice(np.array([0, 1, 18, 40, V - 1]), (N, 4, 16, V)), V); b[:, 4:, :, :48] = V
    return pack(b, x, lm)
def setup_inputs_alike(rng):
    b, x, lm = parts(rng)
    u = rng.random((N, 8, 3, V)); few = np.minimum((V * u * u).astype(np.int64), V - 1)
    few[:, :, 0] = np.where(rng.random((N, 8, V)) < 0.15, np.arange(V), few[:, :, 0])
    pool = rng.integers(V // 2, V, (8, 4)); few[:, :, 2] = pool[np.arange(8)[None, :, None], rng.integers(0, 4, (N, 8, V))]
    which = np.minimum(rng.integers(0, 3, (N, 8, 16, V)), rng.integers(0, 3, (N, 8, 1, V)))
    b = np.where(rng.random((N, 8, 16, V)) < rng.choice(np.array([0.4, 0.8, 1.0]), (N, 8, 1, V)), np.take_along_axis(few, which, 2), V)
    lm = np.minimum(4 * lm, 4079)
    late(rng, b, x, lm, int(rng.integers(0, 8)))
    return pack(b, x, lm)
def check_inputs(d):
    bad = []
    for k, lo, hi in (("nb", 0, V), ("xs", 0, 255), ("lim", 0, 4079)):
        a = np.asarray(d[k]).astype(np.float64)
        if not np.all((a >= lo) & (a <= hi)): bad.append("range of " + k)
        elif not np.all(a == np.floor(a)): bad.append("whole numbers in " + k)
    return bad
def reference(nb, xs, lim):
    b = nb.astype(np.int32).reshape(N, 8, 16, V); x = xs.astype(np.float32).astype(np.int32).reshape(N, 8, 16, V)
    lm = lim.astype(np.int64).reshape(N, 8, 16, 1)
    J = np.tile(np.arange(V), (8, 1)); gone = np.zeros((8, V), bool)
    A = [0] * N; g8 = np.arange(8)[:, None, None]
    for t in range(R):
        new = []
        for r in range(N):
            v = lanes(t, r); q = b[r][:, :, v]
            has = q < V; u = np.where(has, q, 0)
            n = J[g8, u]; elem = has & gone[g8, u]; var = has & ~elem
            at = n.reshape(8, 1, 16 * L)
            Q = np.take_along_axis(b[r], at, 2).reshape(8, 16, 16, L); X = np.take_along_axis(x[r], at, 2).reshape(8, 16, 16, L)
            ek = elem[:, None]
            cov = var & np.any((Q == q[:, :, None, :]) & ek, axis=2)
            unc = var & ~cov
            deg = np.sum(np.where(unc[:, None], X, 0), axis=2) + np.max(np.where(ek, X, 0), axis=2)
            live = ~gone[:, v]
            hit = live & (np.sum(deg <= lm[r] + (A[r] & 7), axis=1) >= 9)
            piv = hit & (np.add.accumulate(hit.astype(np.int64), axis=1) <= CAP)
            col = np.minimum(np.where(unc & (q != v), q, V), np.min(np.where(ek & (Q != v), Q, V), axis=2))
            S = np.where(elem, np.sum(X, axis=1), -1); k = np.argmax(S, axis=1)
            e = np.take_along_axis(n, k[:, None, :], 1)[:, 0, :]
            b[r][:, :, v] = np.where(cov & (live & ~piv)[:, None, :], V, q)
            new.append((v, piv, col, np.minimum(deg, 255), e, piv & np.any(elem, axis=1)))
        for g in range(8):
            es = []; vs = []
            for v, piv, col, sz, e, cl in new:
                w = np.flatnonzero(piv[g]); b[:, g][:, :, v[w]] = col[g][:, w]; x[:, g][:, :, v[w]] = sz[g][:, w]; gone[g, v[w]] = True
                w = np.flatnonzero(cl[g]); es.append(e[g][w]); vs.append(v[w])
            ue, ui = np.unique(np.concatenate(es), return_index=True)
            J[g, ue] = np.concatenate(vs)[ui]
            J[g] = J[g][J[g]]
        A = [int(np.sum(a[1])) for a in new]
    return {"yn": b.reshape(N, 128, V).astype(np.float32), "yx": x.reshape(N, 128, V).astype(np.float32).astype(BF), "yj": np.stack([J] * N).astype(np.float32)}

@@ -1,0 +1,454 @@
+from concourse.bass import DstId, RemoteDMATransfer
+from concourse.mybir import AluOpType, AxisListType, ActivationFunctionType
+
+W = 2368
+F, B, I, U = "float32", "bfloat16", "int32", "uint16"
+SCRATCH = {}
+for _names, _w, _d in (
+        ("NB NE XE JT", W, F), ("XS", W, B), ("SA EQ XG XV MX RST", 2048, B), ("SAF QR YJ", 2048, F),
+        ("RSTB Q2 KS CC NS", 512, F), ("KC X2 MM", 512, B), ("ONEB IDB NI I4 BO BO32 TRI HR HT PV PVB", 128, B), ("CMP", 256, B),
+        ("IDF BOF TQ UA UN THR DQ", 128, F), ("SB", 256, F), ("WTS PR", 2, B), ("KB MB", 64, B), ("K4", 32, B),
+        ("PI PA LIMI AI AM", 1, I), ("PF AF LIMA", 1, F), ("COL", 8, F), ("CA CB IO16", 16, F), ("EW EW2 DM", 2, F),
+        ("LT VT0 VT1 QT0 QT1 QT2 QX0 QX1 QX2 QC OWN SZ", 136, F), ("IOW OQ0 OQ1 OQ2 UL JL", 128, U),
+        ("IO32 D2 QM OP NM OH PD TM TM2 JE", 32, F), ("IO64 MF ED EM", 64, F), ("LW UW", 2, U), ("EP L16", 32, U), ("KI K5", 32, I),
+        ("NV0 NV1 NV2 SV0 SV1 SV2 VR1 VR3", 256, U), ("OF0 OF1 OF2 OE1 OE3", 16, U)):
+    for _n in _names.split():
+        SCRATCH[_n] = ("sbuf", [128, _w], _d)
+for _b in range(4):
+    SCRATCH["LD%d" % _b] = ("sbuf", [128, 8, 104], U)
+for _b in range(8):
+    SCRATCH["P%d" % _b] = ("psum", [128, 512], F)
+SEMAPHORES = ["ev", "et", "ea", "eg", "d_x", "d_n0", "d_n1", "d_l", "o_n", "o_x", "o_j0", "o_j1"]
+SEMAPHORES += ["a%d_%d" % (m, r) for m in range(4) for r in range(8)] + ["l%d" % m for m in range(4)]
+NAMES, SIZES, VOFF, EOFF, VREP = 0, 32, 64, 66, 68
+SPAN = [(0, 66), (0, 100), (0, 66), (66, 100)]
+
+
+def rank_program(g, core, T, topo):
+    rank = T.rank_of(core)
+    if rank is None:
+        return
+    A = AluOpType
+    Q = {"v": g.vector, "t": g.tensor, "a": g.scalar, "g": g, "s": g.sync}
+    cnt, wr, rd, nloc = {}, {}, {}, {}
+    known = {q: {} for q in Q}
+
+    def bank(k):
+        return k[0] == "P" and k[1:].isdigit()
+
+    def pre(q, R, Wk):
+        evs = []
+        for k in R:
+            evs += wr.get(k, [])
+            if bank(k):
+                evs += [e for e in rd.get(k, []) if e[0] != q]
+        for k in Wk:
+            part = q == "t" or k[0] == "+"
+            k = k.lstrip("+")
+            evs += [e for e in wr.get(k, []) if not part or e[0] != q] + rd.get(k, [])
+        top = {}
+        for e in evs:
+            top[e[1]] = max(top.get(e[1], 0), e[2])
+        for e in sorted(evs, key=lambda e: -len(e[3])):
+            if top[e[1]] == e[2] and known[q].get(e[1], 0) < e[2]:
+                Q[q].wait_ge(T.sem[e[1]], e[2])
+                for s, n in e[3].items():
+                    known[q][s] = max(known[q].get(s, 0), n)
+                known[q][e[1]] = e[2]
+
+    def post(q, by, sem, n, R, Wk):
+        ck = dict(known[by])
+        ck[sem] = n
+        ev = (q, sem, n, ck)
+        Wk = [k.lstrip("+") for k in Wk]
+        for k in Wk:
+            wr[k] = [ev]
+            rd[k] = []
+        for k in R:
+            if k not in Wk:
+                rd[k] = [e for e in rd.get(k, []) if e[0] != q] + [ev]
+
+    def op(q, f, R, Wk):
+        R, Wk = R.split(), Wk.split()
+        pre(q, R, Wk)
+        cnt[q] = cnt.get(q, 0) + 1
+        f().then_inc(T.sem["e" + q], 1)
+        post(q, q, "e" + q, cnt[q], R, Wk)
+
+    def dma(q, out, in_, sem, R, Wk):
+        R, Wk = R.split(), Wk.split()
+        pre(q, R, Wk)
+        Q[q].dma_start(out, in_).then_inc(T.sem[sem], 16)
+        post(sem, q, sem, 16, R, Wk)
+
+    V = g.vector
+
+    def cp(out, in_, R, Wk):
+        op("v", lambda: V.tensor_copy(out=out, in_=in_), R, Wk)
+
+    def ts(out, in0, s1, o0, R, Wk, s2=None, o1=None):
+        if o1 is None:
+            op("v", lambda: V.tensor_scalar(out=out, in0=in0, scalar1=s1, scalar2=None, op0=o0), R, Wk)
+        else:
+            op("v", lambda: V.tensor_scalar(out=out, in0=in0, scalar1=s1, scalar2=s2, op0=o0, op1=o1), R, Wk)
+
+    def tt(out, in0, in1, o, R, Wk):
+        op("v", lambda: V.tensor_tensor(out=out, in0=in0, in1=in1, op=o), R, Wk)
+
+    def red(out, in_, o, R, Wk):
+        op("v", lambda: V.tensor_reduce(out=out, in_=in_, axis=AxisListType.X, op=o), R, Wk)
+
+    def scan(out, d0, d1, init, o0, o1, R, Wk):
+        op("v", lambda: V.tensor_tensor_scan(out=out, data0=d0, data1=d1, initial=init, op0=o0, op1=o1), R, Wk)
+
+    def fill(ap, c, Wk):
+        op("v", lambda: V.memset(ap, c), "", Wk)
+
+    def mm(out, l, r, start, stop, R, Wk):
+        op("t", lambda: g.tensor.matmul(out=out, lhsT=l, rhs=r, start=start, stop=stop), R, Wk)
+
+    def act(out, in_, R, Wk, func=ActivationFunctionType.Copy, bias=0.0):
+        op("a", lambda: g.scalar.activation(out=out, in_=in_, func=func, bias=bias), R, Wk)
+
+    def iota(out, pat, base, cm, Wk):
+        op("g", lambda: g.iota(out, pat, base, cm, allow_small_or_imprecise_dtypes=True), "", Wk)
+
+    def asel(out, in_, pat, o, fl, base, cm, R, Wk):
+        op("g", lambda: g.affine_select(out, in_, pat, o, fl, base, cm), R, Wk)
+
+    cls = [rank, 8 + rank, rank]
+    VTs = ["VT0", "VT1", "VT0"]
+
+    dma("s", T.NB[:, 16:1040], T.nb[:, 0:1024], "d_n0", "", "NB0")
+    dma("a", T.XS[:, 16:2064], T.xs[:, :], "d_x", "", "XS")
+    dma("s", T.NB[:, 1040:2064], T.nb[:, 1024:2048], "d_n1", "", "NB1")
+    dma("s", T.LIMI[:, :], T.lim[:, :], "d_l", "", "LIMI")
+
+    fill(T.ONEB[:, :], 1.0, "ONEB")
+    fill(T.WTS[:, 0:1], 1.0, "+WTS")
+    fill(T.WTS[:, 1:2], 16.0, "+WTS")
+    fill(T.XS[:, 0:16], 0.0, "+XSp")
+    fill(T.XS[:, 2064:W], 0.0, "+XSp")
+    asel(T.IDB[:, :], T.ONEB[:, :], [[-1, 128]], A.is_equal, 0.0, 0, 1, "ONEB", "IDB")
+    asel(T.BO[:, :], T.ONEB[:, :], [[-16, 8], [0, 16]], A.is_ge, 0.0, 0, 1, "ONEB", "BO")
+    asel(T.BO[:, :], T.BO[:, :], [[16, 8], [0, 16]], A.is_ge, 0.0, 15, -1, "BO", "BO")
+    asel(T.TRI[:, :], T.ONEB[:, :], [[1, 128]], A.is_ge, 0.0, 0, -1, "ONEB", "TRI")
+    asel(T.WTS[:, 1:2], T.WTS[:, 1:2], [[0, 1]], A.not_equal, 384.0, -127, 1, "WTS", "WTS")
+    op("g", lambda: g.iota(T.PI[:, :], [[0, 1]], 0, 1), "", "PI")
+    iota(T.VT0[:, :], [[16, 136]], cls[0], 0, "VT0")
+    iota(T.SB[:, :], [[16, 2], [0, 8], [1, 16]], 0, 0, "SB")
+    iota(T.IO16[:, :], [[1, 16]], 0, 0, "IO16")
+    iota(T.IO32[:, :], [[0, 2], [1, 16]], 0, 0, "IO32")
+    iota(T.IO64[:, :], [[-16, 2], [1, 32]], 0, 0, "IO64")
+    iota(T.LT[:, :], [[1, 136]], 0, 0, "LT")
+    iota(T.VT1[:, :], [[16, 136]], cls[1], 0, "VT1")
+    iota(T.KC[:, :], [[0, 32], [-1, 16]], 31, 0, "KC")
+    iota(T.NE[:, :], [[0, W]], 2048, 0, "NE")
+    for n in ("QT0", "QT1", "QT2"):
+        fill(T[n][:, 128:136], 2048.0, n + "p")
+    for n in ("QX0", "OWN"):
+        fill(T[n][:, 128:136], 4096.0, n + "p")
+    fill(T.SZ[:, 128:136], 0.0, "SZp")
+    fill(T.KB[:, :], 131072.0, "KB")
+    fill(T.K4[:, :], 4096.0, "K4")
+    fill(T.RST[:, :], 1.0, "RST")
+    fill(T.RST[:, 0:2048:16], 0.0, "RST")
+    fill(T.RSTB[:, :], 0.0, "RSTB")
+    fill(T.RSTB[:, 0:512:16], 8192.0, "RSTB")
+    ts(T.PA[:, :], T.PI[:, :], 15, A.bitwise_and, "PI", "PA")
+    cp(T.PF[:, :], T.PA[:, :], "PA", "PF")
+    ts(T.COL[:, 0:1], T.PF[:, :], -1.0, A.mult, "PF", "+COL", 31.0, A.add)
+    for j, b in enumerate((2080 + 32 * rank, 2096 + 32 * rank, 2336, 2352)):
+        ts(T.COL[:, j + 1:j + 2], T.PF[:, :], float(b), A.add, "PF", "+COL")
+    CODE, TRV, TRE = T.COL[:, 0:1], [T.COL[:, 1:2], T.COL[:, 2:3]], [T.COL[:, 3:4], T.COL[:, 4:5]]
+    ts(T.CA[:, :], T.IO16[:, :], T.PF[:, 0:1], A.is_equal, "IO16 PF", "CA", 131072.0, A.mult)
+    ts(T.NI[:, :], T.IDB[:, :], -4096.0, A.mult, "IDB", "NI")
+    cp(T.IDF[:, :], T.IDB[:, :], "IDB", "IDF")
+    for k in range(16):
+        ts(T.SA[:, 128 * k:128 * k + 128], T.IDB[:, :], T.CA[:, k:k + 1], A.mult, "IDB CA", "+SA")
+    ts(T.BO32[:, :], T.BO[:, :], 32.0, A.mult, "BO", "BO32")
+    ts(T.I4[:, :], T.IDB[:, :], 4096.0, A.mult, "IDB", "I4")
+    ts(T.D2[:, :], T.IO32[:, :], T.PF[:, 0:1], A.is_equal, "IO32 PF", "D2")
+    ts(T.MF[:, :], T.IO64[:, :], T.PF[:, 0:1], A.is_ge, "IO64 PF", "MF", 8192.0, A.mult)
+    ts(T.MB[:, :], T.MF[:, :], 4096.0, A.add, "MF", "MB")
+    cp(T.BOF[:, :], T.BO[:, :], "BO", "BOF")
+    cp(T.IOW[:, :], T.LT[:, 0:128], "LT", "IOW")
+    fill(T.XE[:, :], -1.0, "XE")
+
+    def names_of(t, h):
+        a = 16 + 1024 * h + cls[t]
+        return T.NB[:, a:1040 + 1024 * h:16]
+
+    def mine(m, a, n):
+        return T["LD%d" % m][:, rank, a:a + n]
+
+    def self_out(t):
+        n, vt, qt = "QX%d" % t, VTs[t], "QT%d" % t
+        tt(T.TQ[:, :], T[qt][:, 0:128], T[vt][:, 0:128], A.is_equal, qt + " " + vt, "TQ")
+        ts(T.TQ[:, :], T.TQ[:, :], 4096.0, A.mult, "TQ", "TQ")
+        tt(T[n][:, 0:128], T.TQ[:, :], T[qt][:, 0:128], A.max, "TQ " + qt, n)
+
+    def repeat_names(t):
+        qt = "QT%d" % t
+        ts(T.TQ[:, :], T[qt][:, 0:128], 2048.0, A.is_equal, qt, "TQ", 2048.0, A.mult)
+        tt(T.QC[:, 0:128], T.TQ[:, :], T[qt][:, 0:128], A.add, "TQ " + qt, "QC")
+        act(T.QR[:, :], T.QC[:, 0:128].indirect(T.IOW[:, :]), "QC IOW", "QR")
+
+    def gather_sizes(q, lst, a, b):
+        f = cp if q == "v" else act
+        f(T.XV[:, 16 * a:16 * b], T.XS[:, 0:2080].indirect(T[lst][:, a:b]), "XS XSp " + lst + ("_0" if b <= 64 else "_1"), "XV%d" % a)
+
+    def degrees(h, keys, mx):
+        o = T.P2[:, 64 * h:64 * h + 64]
+        if mx:
+            mm(o, T.IDB[:, :], T.MX[:, 1024 * h + 15:1024 * h + 1024:16], True, False, "IDB MX", "P2")
+        for k in range(16):
+            mm(o, T.IDB[:, :], T.XV[:, 1024 * h + k:1024 * h + 1024:16], k == 0 and not mx, k == 15, "IDB " + keys, "P2")
+
+    def select(t):
+        ts(T.HR[:, :], T.P2[:, 0:128], T.LIMA[:, 0:1], A.is_le, "P2 LIMA", "HR")
+        mm(T.P3[:, 0:128], T.HR[:, :], T.BO[:, :], True, True, "HR BO", "P3")
+        ts(T.SZ[:, 0:128], T.P2[:, 0:128], 255.0, A.min, "P2", "SZ")
+        if t < 2:
+            ts(T.HT[:, :], T.P3[:, 0:128], 9.0, A.is_ge, "P3", "HT")
+        else:
+            tt(T.HT[:, :], T.P3[:, 0:128], T.THR[:, :], A.is_ge, "P3 THR", "HT")
+        for b in range(2):
+            mm(T.P4[:, 128 * b:128 * b + 128], T.TRI[:, :], T.HT[:, :], True, True, "TRI HT", "P4")
+        tt(T.CMP[:, :], T.P4[:, 0:256], T.SB[:, :], A.is_le, "P4 SB", "CMP")
+        for b in range(2):
+            mm(T.P5[:, 2 * b:2 * b + 2], T.CMP[:, 128 * b:128 * b + 128], T.WTS[:, :], True, True, "CMP WTS", "P5")
+        cp(T.LW[:, :], T.P5[:, 0:4:2], "P5", "LW")
+
+    def places(t):
+        for b in range(2):
+            ts(mine(t, VOFF + b, 1), T.P5[:, 2 * b + 1:2 * b + 2], float(cls[t] + 16), A.add, "P5 COL", "+M%d" % t, TRV[b], A.min)
+
+    def at_pivots(buf):
+        return T[buf][:, 0:136].indirect(T.LW[:, :])
+
+    near = [c for c in T.cores if topo.chip(c) == topo.chip(core) and c != core]
+    far = [c for c in T.cores if topo.chip(c) != topo.chip(core)]
+    fe = topo.engines(core, far[0])
+    ne = [e for e in topo.engines(core, near[0]) if e not in fe][:2]
+
+    def send(m):
+        a, b = SPAN[m]
+        tr = []
+        for cs, es in ((far, fe), (near, ne)):
+            ids = [DstId(rid=topo.addr(c)[0], pnc=topo.addr(c)[1]) for c in cs]
+            tr.append(RemoteDMATransfer(dst_ids=ids, dma_engine_mask=sum(1 << e for e in es), remote_sem=T.sem["a%d_%d" % (m, rank)],
+                                        srcs=[mine(m, a, b - a)], dsts=[mine(m, a, b - a)] * len(cs)))
+        pre("g", ["M%d" % m], [])
+        g.remote_dma_fused(tr, local_sem=T.sem["l%d" % m])
+        nloc[m] = len(fe) + len(ne)
+        post("l%d" % m, "g", "l%d" % m, nloc[m], ["M%d" % m], [])
+        for r in range(8):
+            if r != rank:
+                wr["LD%d_%d" % (m, r)] = [("r", "a%d_%d" % (m, r), len(ne) if T.cores[r] in near else len(fe), {})]
+
+    def unpack(m, buf, a, n):
+        keys = " ".join("M%d" % m if r == rank else "LD%d_%d" % (m, r) for r in range(8))
+        cp(T["%s%d" % (buf, m)][:, :], T["LD%d" % m][:, :, a:a + n], keys, "%s%d" % (buf, m))
+
+    def pivots(tab, m, val, keys):
+        cp(T[tab][:, 0:W].indirect(T["OF%d" % m][:, :]), T["%s%d" % (val, m)][:, :], "OF%d %s%d" % (m, val, m), keys)
+
+    def winners(tab, m, val):
+        for r in range(7, -1, -1):
+            cp(T[tab][:, 0:W].indirect(T["OE%d" % m][:, 2 * r:2 * r + 2]), T["%s%d" % (val, m)][:, 32 * r:32 * r + 32], "OE%d %s%d" % (m, val, m), tab)
+
+    def update(m):
+        unpack(m, "OF", VOFF, 2)
+        unpack(m, "SV", SIZES, 32)
+        pivots("XE", m, "SV", "XE")
+        if m:
+            unpack(m, "OE", EOFF, 2)
+            winners("XE", m, "SV")
+        unpack(m, "NV", NAMES, 32)
+        pivots("NE", m, "NV", "NE")
+        if m:
+            winners("NE", m, "NV")
+
+    def count():
+        ts(T.PR[:, :], T.P5[:, 0:4:2], 127.5, A.is_le, "P5", "PR")
+        mm(T.P2[:, 0:2], T.ONEB[:, :], T.PR[:, :], True, True, "ONEB PR", "P2")
+        red(T.AF[:, :], T.P2[:, 0:2], A.add, "P2", "AF")
+        cp(T.AI[:, :], T.AF[:, :], "AF", "AI")
+        ts(T.AM[:, :], T.AI[:, :], 7, A.bitwise_and, "AI", "AM")
+        tt(T.LIMA[:, :], T.AM[:, :], T.LIMI[:, :], A.add, "AM LIMI", "LIMA")
+
+    def lanes_to_pivots(t):
+        qt, oq = "QT%d" % t, "OQ%d" % t
+        for h in range(2):
+            s, l = slice(1024 * h, 1024 * h + 1024), slice(64 * h, 64 * h + 64)
+            act(T.XG[:, s], T.XE[:, 0:2080].indirect(T[oq][:, l]), "XE " + oq, "XG%d" % h)
+            tt(T.EQ[:, s], T.NE[:, 0:2080].indirect(T[oq][:, l]), T.QR[:, s], A.is_equal, "NE QR " + oq, "EQ%d" % h)
+        for h in range(2):
+            pb, s = "P%d" % h, 1024 * h
+            o = T[pb][:, 0:64]
+            mm(o, T.IDF[:, :], T[qt][:, 64 * h:64 * h + 64], True, False, "IDF " + qt, pb)
+            mm(o, T.IDB[:, :], T.KB[:, 0:64], False, False, "IDB KB", pb)
+            for k in range(16):
+                mm(o, T.SA[:, 128 * k:128 * k + 128], T.XG[:, s + k:s + 1024:16], False, False, "SA XG%d" % h, pb)
+            for k in range(16):
+                mm(o, T.NI[:, :], T.EQ[:, s + k:s + 1024:16], False, k == 15, "NI EQ%d" % h, pb)
+        ts(T.UL[:, 0:64], T.P0[:, 0:64], 16.0, A.add, "P0", "UL_0", 2064.0, A.min)
+        gather_sizes("a", "UL", 0, 64)
+        scan(T.MX[:, :], T.RST[:, :], T.XG[:, :], 0.0, A.mult, A.max, "RST XG0 XG1", "MX")
+        ts(T.UL[:, 64:128], T.P1[:, 0:64], 16.0, A.add, "P1", "UL_1", 2064.0, A.min)
+        gather_sizes("a", "UL", 64, 80)
+        gather_sizes("v", "UL", 80, 128)
+        degrees(0, "XV0", True)
+        degrees(1, "XV64 XV80", True)
+        for h in range(2):
+            act(T.UA[:, 64 * h:64 * h + 64], T["P%d" % h][:, 0:64], "P%d" % h, "+UA", func=ActivationFunctionType.Abs)
+        mm(T.P6[:, :], T.IDB[:, :], T.KC[:, :], True, False, "IDB KC", "P6")
+        tt(T.OWN[:, 0:128], T.UA[:, :], T["QX%d" % t][:, 0:128], A.max, "UA QX%d" % t, "OWN")
+        select(t)
+        ts(T.EP[:, :], at_pivots(qt), 16.0, A.add, "%s %sp LW" % (qt, qt), "EP")
+        act(T.X2[:, :], T.XE[:, 0:2080].indirect(T.EP[:, :]), "XE EP", "X2")
+        act(T.Q2[:, :], T.NE[:, 0:2080].indirect(T.EP[:, :]), "NE EP", "Q2")
+        mm(T.P6[:, :], T.BO32[:, :], T.X2[:, :], False, True, "BO32 X2", "P6")
+        cp(T.L16[:, :], at_pivots("LT"), "LT LW", "L16")
+        cp(mine(t, SIZES, 32), at_pivots("SZ"), "SZ SZp LW", "+M%d" % t)
+        ts(T.QM[:, :], at_pivots(qt), -4080.0, A.add, "%s %sp LW" % (qt, qt), "QM")
+        cp(T.OP[:, :], at_pivots("OWN"), "OWN OWNp LW", "OP")
+        places(t)
+
+    def win_row(t):
+        scan(T.KS[:, :], T.RST[:, 0:512], T.P6[:, :], 0.0, A.mult, A.max, "RST P6", "KS")
+        cp(T.KI[:, :], T.KS[:, 15:512:16], "KS", "KI")
+        ts(T.K5[:, :], T.KI[:, :], 31, A.bitwise_and, "KI", "K5")
+        ts(T.OH[:, :], T.K5[:, :], CODE, A.is_equal, "K5 COL", "OH")
+        tt(T.PD[:, :], T.OH[:, :], T.QM[:, :], A.mult, "OH QM", "PD")
+        mm(T.P3[:, 0:32], T.IDB[:, :], T.K4[:, :], True, False, "IDB K4", "P3")
+        mm(T.P3[:, 0:32], T.BOF[:, :], T.PD[:, :], False, True, "BOF PD", "P3")
+        for b in range(2 if t == 1 else 0):
+            o = T.P4[:, 32 * b:32 * b + 32]
+            mm(o, T.IDB[:, :], T.MB[:, 32 * b:32 * b + 32], True, False, "IDB MB", "P4")
+            mm(o, T.BOF[:, :], T.PD[:, :], False, True, "BOF PD", "P4")
+
+    def as_list(rk, rep, tm, ew):
+        tt(T[tm][:, :], rep, T.D2[:, :], A.mult, rk + " D2", tm)
+        for b in range(2):
+            red(T[ew][:, b:b + 1], T[tm][:, 16 * b:16 * b + 16], A.add, tm, "+" + ew)
+
+    def claims(m, em, ek, ew):
+        for b in range(2):
+            ts(T.ED[:, 32 * b:32 * b + 32], em[:, 32 * b:32 * b + 32], T[ew][:, b:b + 1], A.is_equal, ek + " " + ew, "ED%d" % b, 4096.0, A.mult)
+        for b in range(2):
+            red(T.DM[:, b:b + 1], T.ED[:, 32 * b:32 * b + 32], A.max, "ED%d" % b, "DM%d" % b)
+        for b in range(2):
+            ts(mine(m, EOFF + b, 1), T.DM[:, b:b + 1], T[ew][:, b:b + 1], A.max, "DM%d COL %s" % (b, ew), "+M%d" % m, TRE[b], A.min)
+
+    def self_rows(t):
+        vt = VTs[t]
+        tt(T.MM[:, :], T[vt][:, 0:136].indirect(T.L16[:, :]), T.Q2[:, :], A.is_equal, vt + " L16 Q2", "MM")
+        mm(T.P7[:, :], T.I4[:, :], T.MM[:, :], True, True, "I4 MM", "P7")
+
+    def new_names(t):
+        tt(T.CC[:, :], T.Q2[:, :], T.P7[:, :], A.add, "Q2 P7", "CC")
+        scan(T.NS[:, :], T.RSTB[:, :], T.CC[:, :], 8192.0, A.add, A.min, "RSTB CC", "NS")
+        tt(T.NM[:, :], T.NS[:, 15:512:16], T.OP[:, :], A.min, "NS OP", "NM")
+        ts(mine(t, NAMES, 32), T.NM[:, :], 2048.0, A.min, "NM", "+M%d" % t)
+
+    def empty_covered(t):
+        for h in range(2):
+            ts(T.UN[:, 64 * h:64 * h + 64], T["P%d" % h][:, 0:64], 0.0, A.is_lt, "P%d" % h, "+UN", 2048.0, A.mult)
+        for h in range(2):
+            tt(names_of(t, h), T.UN[:, 64 * h:64 * h + 64], names_of(t, h), A.max, "UN NB%d" % h, "NB%d" % h)
+
+    for h in range(2):
+        nk, s = "NB%d" % h, slice(64 * h, 64 * h + 64)
+        ts(T.OQ0[:, s], names_of(0, h), 16.0, A.add, nk, "OQ0_%d" % h)
+        gather_sizes("a", "OQ0", 64 * h, 64 * h + 32)
+        gather_sizes("v", "OQ0", 64 * h + 32, 64 * h + 64)
+        degrees(h, "XV%d XV%d" % (64 * h, 64 * h + 32), False)
+        cp(T.QT0[:, s], names_of(0, h), nk, "+QT0")
+    self_out(0)
+    cp(T.LIMA[:, :], T.LIMI[:, :], "LIMI", "LIMA")
+    select(0)
+    ts(mine(0, NAMES, 32), at_pivots("QX0"), 2048.0, A.min, "QX0 QX0p LW", "+M0")
+    cp(mine(0, SIZES, 32), at_pivots("SZ"), "SZ SZp LW", "+M0")
+    places(0)
+    send(0)
+
+    for h in range(2):
+        cp(T.QT1[:, 64 * h:64 * h + 64], names_of(1, h), "NB%d" % h, "+QT1")
+    repeat_names(1)
+    ts(T.OQ1[:, :], T.QT1[:, 0:128], 16.0, A.add, "QT1", "OQ1")
+    count()
+    ts(T.PV[:, :], T.P4[:, 0:128], 32.0, A.is_le, "P4", "PV")
+    tt(T.PVB[:, :], T.PV[:, :], T.HT[:, :], A.mult, "PV HT", "PVB")
+    mm(T.P7[:, 0:128], T.PVB[:, :], T.IDB[:, :], True, True, "PVB IDB", "P7")
+    ts(T.THR[:, :], T.PVB[:, :], 100.0, A.mult, "PVB", "THR", 9.0, A.add)
+    self_out(1)
+    ts(T.DQ[:, :], T.P7[:, 0:128], 2048.0, A.mult, "P7", "DQ")
+    tt(T.QT2[:, 0:128], T.DQ[:, :], T.QT0[:, 0:128], A.max, "DQ QT0", "QT2")
+    ts(T.OQ2[:, :], T.QT2[:, 0:128], 16.0, A.add, "QT2", "OQ2")
+    iota(T.JT[:, 0:2064], [[1, 2064]], 0, 0, "JT")
+    iota(T.JT[:, 2064:2072], [[0, 8]], 4096, 0, "+JT")
+
+    update(0)
+    lanes_to_pivots(1)
+    win_row(1)
+    self_rows(1)
+    ts(mine(1, VREP, 32), at_pivots("VT1"), 16.0, A.add, "VT1 LW", "+M1")
+    as_list("P3", T.P3[:, 0:32], "TM", "EW")
+    new_names(1)
+    claims(1, T.P4, "P4", "EW")
+    send(1)
+    repeat_names(2)
+    count()
+    empty_covered(1)
+    pivots("NB", 0, "NV", "NB0 NB1")
+    self_out(2)
+    pivots("XS", 0, "SV", "XS")
+
+    update(1)
+    lanes_to_pivots(2)
+    self_rows(2)
+    new_names(2)
+    send(2)
+    unpack(1, "VR", VREP, 32)
+    winners("JT", 1, "VR")
+    ts(mine(3, VREP, 32), at_pivots("VT0"), 16.0, A.add, "VT0 LW", "+M3")
+    win_row(2)
+    as_list("P3", T.P3[:, 0:32], "TM", "EW")
+    ts(T.UW[:, :], T.EW[:, :], 2064.0, A.min, "EW", "UW")
+    cp(T.JE[:, :], T.JT[:, 0:2072].indirect(T.UW[:, :]), "JT UW", "JE")
+    as_list("JE", T.JE[:, :], "TM2", "EW2")
+    for b in range(2):
+        tt(T.EM[:, 32 * b:32 * b + 32], T.JE[:, :], T.MF[:, 32 * b:32 * b + 32], A.add, "JE MF", "+EM")
+    claims(3, T.EM, "EM", "EW2")
+    send(3)
+    ts(T.CB[:, :], T.CA[:, :], 1.0 / 131072.0, A.mult, "CA", "CB")
+    for k in range(16):
+        ts(T.SAF[:, 128 * k:128 * k + 128], T.IDF[:, :], T.CB[:, k:k + 1], A.mult, "IDF CB", "SAF%d" % k)
+        mm(T.P5[:, 0:128], T.SAF[:, 128 * k:128 * k + 128], T.JT[:, 16 + k:2064:16], k == 0, k == 15, "SAF%d JT" % k, "P5")
+    empty_covered(2)
+    pivots("NB", 1, "NV", "NB0 NB1")
+    pivots("XS", 1, "SV", "XS")
+    unpack(2, "OF", VOFF, 2)
+    unpack(2, "NV", NAMES, 32)
+    pivots("NB", 2, "NV", "NB0 NB1")
+    dma("s", T.yn[:, :], T.NB[:, 16:2064], "o_n", "NB0 NB1", "")
+    unpack(2, "SV", SIZES, 32)
+    pivots("XS", 2, "SV", "XS")
+    dma("s", T.yx[:, :], T.XS[:, 16:2064], "o_x", "XS", "")
+    cp(T.JL[:, :], T.P5[:, 0:128], "P5", "JL")
+    unpack(3, "OE", EOFF, 2)
+    unpack(3, "VR", VREP, 32)
+    winners("JT", 3, "VR")
+    act(T.YJ[:, 0:1024], T.JT[:, 0:2072].indirect(T.JL[:, 0:64]), "JT JL", "YJ0", func=ActivationFunctionType.Identity, bias=-16.0)
+    ts(T.YJ[:, 1024:2048], T.JT[:, 0:2072].indirect(T.JL[:, 64:128]), -16.0, A.add, "JT JL", "YJ1")
+    dma("a", T.yj[:, 0:1024], T.YJ[0:128:16, 0:1024], "o_j0", "YJ0", "")
+    dma("s", T.yj[:, 1024:2048], T.YJ[0:128:16, 1024:2048], "o_j1", "YJ1", "")
+
+    for q in ("v", "t", "a", "g"):
+        g.wait_ge(T.sem["e" + q], cnt[q])
+    for s in ("d_x", "d_n0", "d_n1", "d_l", "o_n", "o_x", "o_j0", "o_j1"):
+        g.wait_ge(T.sem[s], 16)
+    for m in range(4):
+        g.wait_ge(T.sem["l%d" % m], nloc[m])

@@ -5,23 +5,23 @@ W = 2368
 F, B, I, U = "float32", "bfloat16", "int32", "uint16"
 SCRATCH = {}
 for _names, _w, _d in (
-        ("NB NE XE JT", W, F), ("XS", W, B), ("SA EQ XG XV MX RST", 2048, B), ("SAF QR YJ", 2048, F),
-        ("RSTB Q2 KS CC NS", 512, F), ("KC X2 MM", 512, B), ("ONEB IDB NI I4 BO BO32 TRI HR HT PV PVB", 128, B), ("CMP", 256, B),
+        ("NB NE XE JT", W, F), ("XS", W, B), ("SA EQ XG XV MX RSM", 2048, B), ("SAF QR YJ", 2048, F),
+        ("RSTB Q2 KS CC NS", 512, F), ("KC X2 MM RST", 512, B), ("ONEB IDB NI I4 BO BO32 TRI HR HT PV PVB", 128, B), ("CMP", 256, B),
         ("IDF BOF TQ UA UN THR DQ", 128, F), ("SB", 256, F), ("WTS PR", 2, B), ("KB MB", 64, B), ("K4", 32, B),
-        ("PI PA LIMI AI AM", 1, I), ("PF AF LIMA", 1, F), ("COL", 8, F), ("CA CB IO16", 16, F), ("EW EW2 DM", 2, F),
+        ("PI PA LIMI AI AM", 1, I), ("PF AF LIMA", 1, F), ("COL", 8, F), ("CA CB IO16", 16, F),
         ("LT VT0 VT1 QT0 QT1 QT2 QX0 QX1 QX2 QC OWN SZ", 136, F), ("IOW OQ0 OQ1 OQ2 UL JL", 128, U),
-        ("IO32 D2 QM OP NM OH PD TM TM2 JE", 32, F), ("IO64 MF ED EM", 64, F), ("LW UW", 2, U), ("EP L16", 32, U), ("KI K5", 32, I),
-        ("NV0 NV1 NV2 SV0 SV1 SV2 VR1 VR3", 256, U), ("OF0 OF1 OF2 OE1 OE3", 16, U)):
+        ("IO32 D2 QM OP NM OH PD TM TM2 TL TL2 JE", 32, F), ("IO64 MF ED EM DX R32", 64, F), ("LW UW", 2, U), ("EP L16", 32, U), ("KI K5", 32, I),
+        ("NV0 NV1 NV2 SV0 SV1 SV2 VR3 VR4", 256, U), ("OF0 OF1 OF2 OE3 OE4", 16, U)):
     for _n in _names.split():
         SCRATCH[_n] = ("sbuf", [128, _w], _d)
-for _b in range(4):
+for _b in range(5):
     SCRATCH["LD%d" % _b] = ("sbuf", [128, 8, 104], U)
 for _b in range(8):
     SCRATCH["P%d" % _b] = ("psum", [128, 512], F)
 SEMAPHORES = ["ev", "et", "ea", "eg", "d_x", "d_n0", "d_n1", "d_l", "o_n", "o_x", "o_j0", "o_j1"]
-SEMAPHORES += ["a%d_%d" % (m, r) for m in range(4) for r in range(8)] + ["l%d" % m for m in range(4)]
+SEMAPHORES += ["a%d_%d" % (m, r) for m in range(5) for r in range(8)] + ["l%d" % m for m in range(5)]
 NAMES, SIZES, VOFF, EOFF, VREP = 0, 32, 64, 66, 68
-SPAN = [(0, 66), (0, 100), (0, 66), (66, 100)]
+SPAN = [(0, 66), (0, 66), (0, 66), (66, 100), (66, 100)]
 
 
 def rank_program(g, core, T, topo):
@@ -29,6 +29,7 @@ def rank_program(g, core, T, topo):
     if rank is None:
         return
     A = AluOpType
+    IDN = ActivationFunctionType.Identity
     Q = {"v": g.vector, "t": g.tensor, "a": g.scalar, "g": g, "s": g.sync}
     cnt, wr, rd, nloc = {}, {}, {}, {}
     known = {q: {} for q in Q}
@@ -107,8 +108,8 @@ def rank_program(g, core, T, topo):
     def mm(out, l, r, start, stop, R, Wk):
         op("t", lambda: g.tensor.matmul(out=out, lhsT=l, rhs=r, start=start, stop=stop), R, Wk)
 
-    def act(out, in_, R, Wk, func=ActivationFunctionType.Copy, bias=0.0):
-        op("a", lambda: g.scalar.activation(out=out, in_=in_, func=func, bias=bias), R, Wk)
+    def act(out, in_, R, Wk, func=ActivationFunctionType.Copy, bias=0.0, scale=1.0):
+        op("a", lambda: g.scalar.activation(out=out, in_=in_, func=func, bias=bias, scale=scale), R, Wk)
 
     def iota(out, pat, base, cm, Wk):
         op("g", lambda: g.iota(out, pat, base, cm, allow_small_or_imprecise_dtypes=True), "", Wk)
@@ -152,7 +153,9 @@ def rank_program(g, core, T, topo):
     fill(T.KB[:, :], 131072.0, "KB")
     fill(T.K4[:, :], 4096.0, "K4")
     fill(T.RST[:, :], 1.0, "RST")
-    fill(T.RST[:, 0:2048:16], 0.0, "RST")
+    fill(T.RST[:, 0:512:16], 0.0, "RST")
+    fill(T.R32[:, :], 1.0, "R32")
+    fill(T.R32[:, 0:64:32], 0.0, "R32")
     fill(T.RSTB[:, :], 0.0, "RSTB")
     fill(T.RSTB[:, 0:512:16], 8192.0, "RSTB")
     ts(T.PA[:, :], T.PI[:, :], 15, A.bitwise_and, "PI", "PA")
@@ -162,10 +165,9 @@ def rank_program(g, core, T, topo):
         ts(T.COL[:, j + 1:j + 2], T.PF[:, :], float(b), A.add, "PF", "+COL")
     CODE, TRV, TRE = T.COL[:, 0:1], [T.COL[:, 1:2], T.COL[:, 2:3]], [T.COL[:, 3:4], T.COL[:, 4:5]]
     ts(T.CA[:, :], T.IO16[:, :], T.PF[:, 0:1], A.is_equal, "IO16 PF", "CA", 131072.0, A.mult)
+    ts(T.CB[:, :], T.IO16[:, :], T.PF[:, 0:1], A.is_equal, "IO16 PF", "CB")
     ts(T.NI[:, :], T.IDB[:, :], -4096.0, A.mult, "IDB", "NI")
     cp(T.IDF[:, :], T.IDB[:, :], "IDB", "IDF")
-    for k in range(16):
-        ts(T.SA[:, 128 * k:128 * k + 128], T.IDB[:, :], T.CA[:, k:k + 1], A.mult, "IDB CA", "+SA")
     ts(T.BO32[:, :], T.BO[:, :], 32.0, A.mult, "BO", "BO32")
     ts(T.I4[:, :], T.IDB[:, :], 4096.0, A.mult, "IDB", "I4")
     ts(T.D2[:, :], T.IO32[:, :], T.PF[:, 0:1], A.is_equal, "IO32 PF", "D2")
@@ -173,7 +175,6 @@ def rank_program(g, core, T, topo):
     ts(T.MB[:, :], T.MF[:, :], 4096.0, A.add, "MF", "MB")
     cp(T.BOF[:, :], T.BO[:, :], "BO", "BOF")
     cp(T.IOW[:, :], T.LT[:, 0:128], "LT", "IOW")
-    fill(T.XE[:, :], -1.0, "XE")
 
     def names_of(t, h):
         a = 16 + 1024 * h + cls[t]
@@ -209,6 +210,8 @@ def rank_program(g, core, T, topo):
         ts(T.HR[:, :], T.P2[:, 0:128], T.LIMA[:, 0:1], A.is_le, "P2 LIMA", "HR")
         mm(T.P3[:, 0:128], T.HR[:, :], T.BO[:, :], True, True, "HR BO", "P3")
         ts(T.SZ[:, 0:128], T.P2[:, 0:128], 255.0, A.min, "P2", "SZ")
+        if t:
+            tt(T.OWN[:, 0:128], T.UA[:, :], T["QX%d" % t][:, 0:128], A.max, "UA QX%d" % t, "OWN")
         if t < 2:
             ts(T.HT[:, :], T.P3[:, 0:128], 9.0, A.is_ge, "P3", "HT")
         else:
@@ -254,21 +257,16 @@ def rank_program(g, core, T, topo):
     def pivots(tab, m, val, keys):
         cp(T[tab][:, 0:W].indirect(T["OF%d" % m][:, :]), T["%s%d" % (val, m)][:, :], "OF%d %s%d" % (m, val, m), keys)
 
-    def winners(tab, m, val):
+    def winners(tab, m, val, vm):
         for r in range(7, -1, -1):
-            cp(T[tab][:, 0:W].indirect(T["OE%d" % m][:, 2 * r:2 * r + 2]), T["%s%d" % (val, m)][:, 32 * r:32 * r + 32], "OE%d %s%d" % (m, val, m), tab)
+            cp(T[tab][:, 0:W].indirect(T["OE%d" % m][:, 2 * r:2 * r + 2]), T["%s%d" % (val, vm)][:, 32 * r:32 * r + 32], "OE%d %s%d" % (m, val, vm), tab)
 
     def update(m):
         unpack(m, "OF", VOFF, 2)
         unpack(m, "SV", SIZES, 32)
         pivots("XE", m, "SV", "XE")
-        if m:
-            unpack(m, "OE", EOFF, 2)
-            winners("XE", m, "SV")
         unpack(m, "NV", NAMES, 32)
         pivots("NE", m, "NV", "NE")
-        if m:
-            winners("NE", m, "NV")
 
     def count():
         ts(T.PR[:, :], T.P5[:, 0:4:2], 127.5, A.is_le, "P5", "PR")
@@ -278,46 +276,68 @@ def rank_program(g, core, T, topo):
         ts(T.AM[:, :], T.AI[:, :], 7, A.bitwise_and, "AI", "AM")
         tt(T.LIMA[:, :], T.AM[:, :], T.LIMI[:, :], A.add, "AM LIMI", "LIMA")
 
+    def empty_covered(t):
+        for h in range(2):
+            ts(T.UN[:, 64 * h:64 * h + 64], T["P%d" % h][:, 0:64], 0.0, A.is_lt, "P%d" % h, "+UN", 2048.0, A.mult)
+        for h in range(2):
+            tt(names_of(t, h), T.UN[:, 64 * h:64 * h + 64], names_of(t, h), A.max, "UN NB%d" % h, "NB%d" % h)
+
     def lanes_to_pivots(t):
         qt, oq = "QT%d" % t, "OQ%d" % t
         for h in range(2):
-            s, l = slice(1024 * h, 1024 * h + 1024), slice(64 * h, 64 * h + 64)
-            act(T.XG[:, s], T.XE[:, 0:2080].indirect(T[oq][:, l]), "XE " + oq, "XG%d" % h)
-            tt(T.EQ[:, s], T.NE[:, 0:2080].indirect(T[oq][:, l]), T.QR[:, s], A.is_equal, "NE QR " + oq, "EQ%d" % h)
+            act(T.XG[:, 1024 * h:1024 * h + 1024], T.XE[:, 0:2080].indirect(T[oq][:, 64 * h:64 * h + 64]), "XE " + oq, "XG%d" % h)
+
+        def cover(a, b, key):
+            tt(T.EQ[:, 16 * a:16 * b], T.NE[:, 0:2080].indirect(T[oq][:, a:b]), T.QR[:, 16 * a:16 * b], A.is_equal, "NE QR " + oq, key)
+        cover(0, 64, "EQ0")
+        cover(64, 96, "EQ1")
+        for h in range(2):
+            o = T["P%d" % h][:, 0:64]
+            mm(o, T.IDF[:, :], T[qt][:, 64 * h:64 * h + 64], True, False, "IDF " + qt, "P%d" % h)
+            mm(o, T.IDB[:, :], T.KB[:, 0:64], False, False, "IDB KB", "P%d" % h)
         for h in range(2):
             pb, s = "P%d" % h, 1024 * h
             o = T[pb][:, 0:64]
-            mm(o, T.IDF[:, :], T[qt][:, 64 * h:64 * h + 64], True, False, "IDF " + qt, pb)
-            mm(o, T.IDB[:, :], T.KB[:, 0:64], False, False, "IDB KB", pb)
+            if h:
+                ts(T.UL[:, 0:64], T.P0[:, 0:64], 16.0, A.add, "P0", "UL_0", 2064.0, A.min)
+                cover(96, 128, "EQ2")
             for k in range(16):
                 mm(o, T.SA[:, 128 * k:128 * k + 128], T.XG[:, s + k:s + 1024:16], False, False, "SA XG%d" % h, pb)
             for k in range(16):
-                mm(o, T.NI[:, :], T.EQ[:, s + k:s + 1024:16], False, k == 15, "NI EQ%d" % h, pb)
-        ts(T.UL[:, 0:64], T.P0[:, 0:64], 16.0, A.add, "P0", "UL_0", 2064.0, A.min)
+                mm(o, T.NI[:, :], T.EQ[:, s + k:s + 1024:16], False, k == 15, "NI " + ("EQ1 EQ2" if h else "EQ0"), pb)
         gather_sizes("a", "UL", 0, 64)
-        scan(T.MX[:, :], T.RST[:, :], T.XG[:, :], 0.0, A.mult, A.max, "RST XG0 XG1", "MX")
+        scan(T.MX[:, :], T.RSM[:, :], T.XG[:, :], 0.0, A.min, A.max, "RSM XG0 XG1", "MX")
         ts(T.UL[:, 64:128], T.P1[:, 0:64], 16.0, A.add, "P1", "UL_1", 2064.0, A.min)
-        gather_sizes("a", "UL", 64, 80)
-        gather_sizes("v", "UL", 80, 128)
+        gather_sizes("a", "UL", 64, 96)
+        gather_sizes("v", "UL", 96, 128)
+        empty_covered(t)
         degrees(0, "XV0", True)
-        degrees(1, "XV64 XV80", True)
+        degrees(1, "XV64 XV96", True)
         for h in range(2):
             act(T.UA[:, 64 * h:64 * h + 64], T["P%d" % h][:, 0:64], "P%d" % h, "+UA", func=ActivationFunctionType.Abs)
         mm(T.P6[:, :], T.IDB[:, :], T.KC[:, :], True, False, "IDB KC", "P6")
-        tt(T.OWN[:, 0:128], T.UA[:, :], T["QX%d" % t][:, 0:128], A.max, "UA QX%d" % t, "OWN")
         select(t)
         ts(T.EP[:, :], at_pivots(qt), 16.0, A.add, "%s %sp LW" % (qt, qt), "EP")
-        act(T.X2[:, :], T.XE[:, 0:2080].indirect(T.EP[:, :]), "XE EP", "X2")
         act(T.Q2[:, :], T.NE[:, 0:2080].indirect(T.EP[:, :]), "NE EP", "Q2")
-        mm(T.P6[:, :], T.BO32[:, :], T.X2[:, :], False, True, "BO32 X2", "P6")
+        act(T.X2[:, :], T.XE[:, 0:2080].indirect(T.EP[:, :]), "XE EP", "X2")
         cp(T.L16[:, :], at_pivots("LT"), "LT LW", "L16")
         cp(mine(t, SIZES, 32), at_pivots("SZ"), "SZ SZp LW", "+M%d" % t)
         ts(T.QM[:, :], at_pivots(qt), -4080.0, A.add, "%s %sp LW" % (qt, qt), "QM")
         cp(T.OP[:, :], at_pivots("OWN"), "OWN OWNp LW", "OP")
         places(t)
 
+    def new_names(t):
+        vt = VTs[t]
+        tt(T.MM[:, :], T[vt][:, 0:136].indirect(T.L16[:, :]), T.Q2[:, :], A.is_equal, vt + " L16 Q2", "MM")
+        mm(T.P7[:, :], T.I4[:, :], T.MM[:, :], True, True, "I4 MM", "P7")
+        tt(T.CC[:, :], T.Q2[:, :], T.P7[:, :], A.add, "Q2 P7", "CC")
+        scan(T.NS[:, :], T.RSTB[:, :], T.CC[:, :], 8192.0, A.add, A.min, "RSTB CC", "NS")
+        tt(T.NM[:, :], T.NS[:, 15:512:16], T.OP[:, :], A.min, "NS OP", "NM")
+        ts(mine(t, NAMES, 32), T.NM[:, :], 2048.0, A.min, "NM", "+M%d" % t)
+
     def win_row(t):
-        scan(T.KS[:, :], T.RST[:, 0:512], T.P6[:, :], 0.0, A.mult, A.max, "RST P6", "KS")
+        mm(T.P6[:, :], T.BO32[:, :], T.X2[:, :], False, True, "BO32 X2", "P6")
+        scan(T.KS[:, :], T.RST[:, :], T.P6[:, :], 0.0, A.mult, A.max, "RST P6", "KS")
         cp(T.KI[:, :], T.KS[:, 15:512:16], "KS", "KI")
         ts(T.K5[:, :], T.KI[:, :], 31, A.bitwise_and, "KI", "K5")
         ts(T.OH[:, :], T.K5[:, :], CODE, A.is_equal, "K5 COL", "OH")
@@ -329,35 +349,17 @@ def rank_program(g, core, T, topo):
             mm(o, T.IDB[:, :], T.MB[:, 32 * b:32 * b + 32], True, False, "IDB MB", "P4")
             mm(o, T.BOF[:, :], T.PD[:, :], False, True, "BOF PD", "P4")
 
-    def as_list(rk, rep, tm, ew):
+    def as_list(rk, rep, tm, tl):
         tt(T[tm][:, :], rep, T.D2[:, :], A.mult, rk + " D2", tm)
-        for b in range(2):
-            red(T[ew][:, b:b + 1], T[tm][:, 16 * b:16 * b + 16], A.add, tm, "+" + ew)
+        scan(T[tl][:, :], T.RST[:, 0:32], T[tm][:, :], 0.0, A.mult, A.add, "RST " + tm, tl)
 
-    def claims(m, em, ek, ew):
+    def claims(m, em, ek, tl):
+        col = [T[tl][:, 15:16], T[tl][:, 31:32]]
         for b in range(2):
-            ts(T.ED[:, 32 * b:32 * b + 32], em[:, 32 * b:32 * b + 32], T[ew][:, b:b + 1], A.is_equal, ek + " " + ew, "ED%d" % b, 4096.0, A.mult)
+            ts(T.ED[:, 32 * b:32 * b + 32], em[:, 32 * b:32 * b + 32], col[b], A.is_equal, ek + " " + tl, "+ED", 4096.0, A.mult)
+        scan(T.DX[:, :], T.R32[:, :], T.ED[:, :], 0.0, A.mult, A.max, "R32 ED", "DX")
         for b in range(2):
-            red(T.DM[:, b:b + 1], T.ED[:, 32 * b:32 * b + 32], A.max, "ED%d" % b, "DM%d" % b)
-        for b in range(2):
-            ts(mine(m, EOFF + b, 1), T.DM[:, b:b + 1], T[ew][:, b:b + 1], A.max, "DM%d COL %s" % (b, ew), "+M%d" % m, TRE[b], A.min)
-
-    def self_rows(t):
-        vt = VTs[t]
-        tt(T.MM[:, :], T[vt][:, 0:136].indirect(T.L16[:, :]), T.Q2[:, :], A.is_equal, vt + " L16 Q2", "MM")
-        mm(T.P7[:, :], T.I4[:, :], T.MM[:, :], True, True, "I4 MM", "P7")
-
-    def new_names(t):
-        tt(T.CC[:, :], T.Q2[:, :], T.P7[:, :], A.add, "Q2 P7", "CC")
-        scan(T.NS[:, :], T.RSTB[:, :], T.CC[:, :], 8192.0, A.add, A.min, "RSTB CC", "NS")
-        tt(T.NM[:, :], T.NS[:, 15:512:16], T.OP[:, :], A.min, "NS OP", "NM")
-        ts(mine(t, NAMES, 32), T.NM[:, :], 2048.0, A.min, "NM", "+M%d" % t)
-
-    def empty_covered(t):
-        for h in range(2):
-            ts(T.UN[:, 64 * h:64 * h + 64], T["P%d" % h][:, 0:64], 0.0, A.is_lt, "P%d" % h, "+UN", 2048.0, A.mult)
-        for h in range(2):
-            tt(names_of(t, h), T.UN[:, 64 * h:64 * h + 64], names_of(t, h), A.max, "UN NB%d" % h, "NB%d" % h)
+            ts(mine(m, EOFF + b, 1), T.DX[:, 32 * b + 31:32 * b + 32], col[b], A.max, "DX COL " + tl, "+M%d" % m, TRE[b], A.min)
 
     for h in range(2):
         nk, s = "NB%d" % h, slice(64 * h, 64 * h + 64)
@@ -366,6 +368,9 @@ def rank_program(g, core, T, topo):
         gather_sizes("v", "OQ0", 64 * h + 32, 64 * h + 64)
         degrees(h, "XV%d XV%d" % (64 * h, 64 * h + 32), False)
         cp(T.QT0[:, s], names_of(0, h), nk, "+QT0")
+    act(T.XE[:, :], T.NE[:, :], "NE", "XE", func=IDN, bias=-1.0, scale=0.0)
+    for k in range(16):
+        act(T.SA[:, 128 * k:128 * k + 128], T.IDB[:, :], "IDB CA", "+SA", scale=T.CA[:, k:k + 1])
     self_out(0)
     cp(T.LIMA[:, :], T.LIMI[:, :], "LIMI", "LIMA")
     select(0)
@@ -387,61 +392,62 @@ def rank_program(g, core, T, topo):
     ts(T.DQ[:, :], T.P7[:, 0:128], 2048.0, A.mult, "P7", "DQ")
     tt(T.QT2[:, 0:128], T.DQ[:, :], T.QT0[:, 0:128], A.max, "DQ QT0", "QT2")
     ts(T.OQ2[:, :], T.QT2[:, 0:128], 16.0, A.add, "QT2", "OQ2")
+    self_out(2)
+    iota(T.RSM[:, :], [[0, 128], [256, 16]], 0, 0, "RSM")
     iota(T.JT[:, 0:2064], [[1, 2064]], 0, 0, "JT")
     iota(T.JT[:, 2064:2072], [[0, 8]], 4096, 0, "+JT")
 
     update(0)
     lanes_to_pivots(1)
-    win_row(1)
-    self_rows(1)
-    ts(mine(1, VREP, 32), at_pivots("VT1"), 16.0, A.add, "VT1 LW", "+M1")
-    as_list("P3", T.P3[:, 0:32], "TM", "EW")
     new_names(1)
-    claims(1, T.P4, "P4", "EW")
     send(1)
+    ts(mine(4, VREP, 32), at_pivots("VT1"), 16.0, A.add, "VT1 LW", "+M4")
+    win_row(1)
+    as_list("P3", T.P3[:, 0:32], "TM", "TL")
+    claims(4, T.P4, "P4", "TL")
+    send(4)
     repeat_names(2)
+    for k in range(16):
+        act(T.SAF[:, 128 * k:128 * k + 128], T.IDF[:, :], "IDF CB", "+SAF", scale=T.CB[:, k:k + 1])
     count()
-    empty_covered(1)
     pivots("NB", 0, "NV", "NB0 NB1")
-    self_out(2)
-    pivots("XS", 0, "SV", "XS")
 
     update(1)
+    unpack(4, "OE", EOFF, 2)
+    winners("XE", 4, "SV", 1)
+    winners("NE", 4, "NV", 1)
     lanes_to_pivots(2)
-    self_rows(2)
     new_names(2)
     send(2)
-    unpack(1, "VR", VREP, 32)
-    winners("JT", 1, "VR")
     ts(mine(3, VREP, 32), at_pivots("VT0"), 16.0, A.add, "VT0 LW", "+M3")
     win_row(2)
-    as_list("P3", T.P3[:, 0:32], "TM", "EW")
-    ts(T.UW[:, :], T.EW[:, :], 2064.0, A.min, "EW", "UW")
+    unpack(4, "VR", VREP, 32)
+    winners("JT", 4, "VR", 4)
+    for k in range(16):
+        mm(T.P5[:, 0:128], T.SAF[:, 128 * k:128 * k + 128], T.JT[:, 16 + k:2064:16], k == 0, k == 15, "SAF JT", "P5")
+    as_list("P3", T.P3[:, 0:32], "TM", "TL")
+    ts(T.UW[:, :], T.TL[:, 15:32:16], 2064.0, A.min, "TL", "UW")
     cp(T.JE[:, :], T.JT[:, 0:2072].indirect(T.UW[:, :]), "JT UW", "JE")
-    as_list("JE", T.JE[:, :], "TM2", "EW2")
+    as_list("JE", T.JE[:, :], "TM2", "TL2")
     for b in range(2):
         tt(T.EM[:, 32 * b:32 * b + 32], T.JE[:, :], T.MF[:, 32 * b:32 * b + 32], A.add, "JE MF", "+EM")
-    claims(3, T.EM, "EM", "EW2")
+    claims(3, T.EM, "EM", "TL2")
     send(3)
-    ts(T.CB[:, :], T.CA[:, :], 1.0 / 131072.0, A.mult, "CA", "CB")
-    for k in range(16):
-        ts(T.SAF[:, 128 * k:128 * k + 128], T.IDF[:, :], T.CB[:, k:k + 1], A.mult, "IDF CB", "SAF%d" % k)
-        mm(T.P5[:, 0:128], T.SAF[:, 128 * k:128 * k + 128], T.JT[:, 16 + k:2064:16], k == 0, k == 15, "SAF%d JT" % k, "P5")
-    empty_covered(2)
+
     pivots("NB", 1, "NV", "NB0 NB1")
-    pivots("XS", 1, "SV", "XS")
     unpack(2, "OF", VOFF, 2)
     unpack(2, "NV", NAMES, 32)
     pivots("NB", 2, "NV", "NB0 NB1")
     dma("s", T.yn[:, :], T.NB[:, 16:2064], "o_n", "NB0 NB1", "")
     unpack(2, "SV", SIZES, 32)
-    pivots("XS", 2, "SV", "XS")
+    for m in range(3):
+        pivots("XS", m, "SV", "XS")
     dma("s", T.yx[:, :], T.XS[:, 16:2064], "o_x", "XS", "")
     cp(T.JL[:, :], T.P5[:, 0:128], "P5", "JL")
     unpack(3, "OE", EOFF, 2)
     unpack(3, "VR", VREP, 32)
-    winners("JT", 3, "VR")
-    act(T.YJ[:, 0:1024], T.JT[:, 0:2072].indirect(T.JL[:, 0:64]), "JT JL", "YJ0", func=ActivationFunctionType.Identity, bias=-16.0)
+    winners("JT", 3, "VR", 3)
+    act(T.YJ[:, 0:1024], T.JT[:, 0:2072].indirect(T.JL[:, 0:64]), "JT JL", "YJ0", func=IDN, bias=-16.0)
     ts(T.YJ[:, 1024:2048], T.JT[:, 0:2072].indirect(T.JL[:, 64:128]), -16.0, A.add, "JT JL", "YJ1")
     dma("a", T.yj[:, 0:1024], T.YJ[0:128:16, 0:1024], "o_j0", "YJ0", "")
     dma("s", T.yj[:, 1024:2048], T.YJ[0:128:16, 1024:2048], "o_j1", "YJ1", "")
@@ -450,5 +456,5 @@ def rank_program(g, core, T, topo):
         g.wait_ge(T.sem["e" + q], cnt[q])
     for s in ("d_x", "d_n0", "d_n1", "d_l", "o_n", "o_x", "o_j0", "o_j1"):
         g.wait_ge(T.sem[s], 16)
-    for m in range(4):
+    for m in range(5):
         g.wait_ge(T.sem["l%d" % m], nloc[m])

@@ -5,23 +5,23 @@ W = 2368
 F, B, I, U = "float32", "bfloat16", "int32", "uint16"
 SCRATCH = {}
 for _names, _w, _d in (
-        ("NB NE XE JT", W, F), ("XS", W, B), ("SA EQ XG XV MX RSM", 2048, B), ("SAF QR YJ", 2048, F),
-        ("RSTB Q2 KS CC NS", 512, F), ("KC X2 MM RST", 512, B), ("ONEB IDB NI I4 BO BO32 TRI HR HT PV PVB", 128, B), ("CMP", 256, B),
+        ("NX", 2 * W, F), ("NB JT", W, F), ("XS", W, B), ("SA EQ XG XV MX RSM", 2048, B), ("SAF QR YJ", 2048, F),
+        ("RSTB Q2 KS CC NS", 512, F), ("KC X2 MM RST", 512, B), ("ONEB IDB I4 BO BO32 TRI HR HT PV PVB", 128, B), ("CMP", 256, B),
         ("IDF BOF TQ UA UN THR DQ", 128, F), ("SB", 256, F), ("WTS PR", 2, B), ("KB MB", 64, B), ("K4", 32, B),
-        ("PI PA LIMI AI AM", 1, I), ("PF AF LIMA", 1, F), ("COL", 8, F), ("CA CB IO16", 16, F),
-        ("LT VT0 VT1 QT0 QT1 QT2 QX0 QX1 QX2 QC OWN SZ", 136, F), ("IOW OQ0 OQ1 OQ2 UL JL", 128, U),
+        ("PI PA LIMI AI AM", 1, I), ("PF LIMA", 1, F), ("COL", 8, F), ("CA CB CM CV IO16", 16, F),
+        ("LT VT0 VT1 QT0 QT1 QT2 QX0 QX1 QX2 QC OWN SZ", 136, F), ("OQ0 OQ1 OQ2 UL JL", 128, U),
         ("IO32 D2 QM OP NM OH PD TM TM2 TL TL2 JE", 32, F), ("IO64 MF ED EM DX R32", 64, F), ("LW UW", 2, U), ("EP L16", 32, U), ("KI K5", 32, I),
-        ("NV0 NV1 NV2 SV0 SV1 SV2 VR3 VR4", 256, U), ("OF0 OF1 OF2 OE3 OE4", 16, U)):
+        ("NV0 NV1 NV2 SV0 SV1 SV5", 256, U), ("OF0 OF1 OF5 OE3", 16, U), ("OE4", 32, U)):
     for _n in _names.split():
         SCRATCH[_n] = ("sbuf", [128, _w], _d)
-for _b in range(5):
+for _b in range(6):
     SCRATCH["LD%d" % _b] = ("sbuf", [128, 8, 104], U)
 for _b in range(8):
     SCRATCH["P%d" % _b] = ("psum", [128, 512], F)
-SEMAPHORES = ["ev", "et", "ea", "eg", "d_x", "d_n0", "d_n1", "d_l", "o_n", "o_x", "o_j0", "o_j1"]
-SEMAPHORES += ["a%d_%d" % (m, r) for m in range(5) for r in range(8)] + ["l%d" % m for m in range(5)]
-NAMES, SIZES, VOFF, EOFF, VREP = 0, 32, 64, 66, 68
-SPAN = [(0, 66), (0, 66), (0, 66), (66, 100), (66, 100)]
+SEMAPHORES = ["ev", "et", "ea", "eg", "d_x", "d_n0", "d_n1", "d_n2", "d_l", "o_n", "o_x", "o_j0", "o_j1"]
+SEMAPHORES += ["a%d_%d" % (m, r) for m in range(6) for r in range(8)] + ["l%d" % m for m in range(6)]
+VOFF, SIZES, NAMES, EOFF2, EOFF, VREP = 0, 2, 34, 66, 68, 70
+SPAN = [(0, 66), (0, 66), (34, 66), (68, 102), (66, 102), (0, 34)]
 
 
 def rank_program(g, core, T, topo):
@@ -96,9 +96,6 @@ def rank_program(g, core, T, topo):
     def tt(out, in0, in1, o, R, Wk):
         op("v", lambda: V.tensor_tensor(out=out, in0=in0, in1=in1, op=o), R, Wk)
 
-    def red(out, in_, o, R, Wk):
-        op("v", lambda: V.tensor_reduce(out=out, in_=in_, axis=AxisListType.X, op=o), R, Wk)
-
     def scan(out, d0, d1, init, o0, o1, R, Wk):
         op("v", lambda: V.tensor_tensor_scan(out=out, data0=d0, data1=d1, initial=init, op0=o0, op1=o1), R, Wk)
 
@@ -119,10 +116,14 @@ def rank_program(g, core, T, topo):
 
     cls = [rank, 8 + rank, rank]
     VTs = ["VT0", "VT1", "VT0"]
+    NBK = "NB0 NB1 NB2"
+    TAB = {"NB": T.NB[:, 0:W], "XS": T.XS[:, 0:W], "NE": T.NX[:, 0:W], "XE": T.NX[:, W:2 * W], "JT": T.JT[:, 0:W]}
+    NEW, XEW = T.NX[:, 0:2080], T.NX[:, W:W + 2080]
 
     dma("s", T.NB[:, 16:1040], T.nb[:, 0:1024], "d_n0", "", "NB0")
     dma("a", T.XS[:, 16:2064], T.xs[:, :], "d_x", "", "XS")
-    dma("s", T.NB[:, 1040:2064], T.nb[:, 1024:2048], "d_n1", "", "NB1")
+    dma("s", T.NB[:, 1040:1552], T.nb[:, 1024:1536], "d_n1", "", "NB1")
+    dma("s", T.NB[:, 1552:2064], T.nb[:, 1536:2048], "d_n2", "", "NB2")
     dma("s", T.LIMI[:, :], T.lim[:, :], "d_l", "", "LIMI")
 
     fill(T.ONEB[:, :], 1.0, "ONEB")
@@ -144,7 +145,7 @@ def rank_program(g, core, T, topo):
     iota(T.LT[:, :], [[1, 136]], 0, 0, "LT")
     iota(T.VT1[:, :], [[16, 136]], cls[1], 0, "VT1")
     iota(T.KC[:, :], [[0, 32], [-1, 16]], 31, 0, "KC")
-    iota(T.NE[:, :], [[0, W]], 2048, 0, "NE")
+    iota(T.NX[:, 0:W], [[0, W]], 2050, 0, "NE")
     for n in ("QT0", "QT1", "QT2"):
         fill(T[n][:, 128:136], 2048.0, n + "p")
     for n in ("QX0", "OWN"):
@@ -164,9 +165,10 @@ def rank_program(g, core, T, topo):
     for j, b in enumerate((2080 + 32 * rank, 2096 + 32 * rank, 2336, 2352)):
         ts(T.COL[:, j + 1:j + 2], T.PF[:, :], float(b), A.add, "PF", "+COL")
     CODE, TRV, TRE = T.COL[:, 0:1], [T.COL[:, 1:2], T.COL[:, 2:3]], [T.COL[:, 3:4], T.COL[:, 4:5]]
-    ts(T.CA[:, :], T.IO16[:, :], T.PF[:, 0:1], A.is_equal, "IO16 PF", "CA", 131072.0, A.mult)
     ts(T.CB[:, :], T.IO16[:, :], T.PF[:, 0:1], A.is_equal, "IO16 PF", "CB")
-    ts(T.NI[:, :], T.IDB[:, :], -4096.0, A.mult, "IDB", "NI")
+    ts(T.CM[:, :], T.IO16[:, :], T.PF[:, 0:1], A.not_equal, "IO16 PF", "CM")
+    ts(T.CV[:, :], T.CB[:, :], 2050.0, A.mult, "CB", "CV")
+    ts(T.CA[:, :], T.CB[:, :], -126976.0, A.mult, "CB", "CA", -4096.0, A.add)
     cp(T.IDF[:, :], T.IDB[:, :], "IDB", "IDF")
     ts(T.BO32[:, :], T.BO[:, :], 32.0, A.mult, "BO", "BO32")
     ts(T.I4[:, :], T.IDB[:, :], 4096.0, A.mult, "IDB", "I4")
@@ -174,14 +176,15 @@ def rank_program(g, core, T, topo):
     ts(T.MF[:, :], T.IO64[:, :], T.PF[:, 0:1], A.is_ge, "IO64 PF", "MF", 8192.0, A.mult)
     ts(T.MB[:, :], T.MF[:, :], 4096.0, A.add, "MF", "MB")
     cp(T.BOF[:, :], T.BO[:, :], "BO", "BOF")
-    cp(T.IOW[:, :], T.LT[:, 0:128], "LT", "IOW")
 
-    def names_of(t, h):
-        a = 16 + 1024 * h + cls[t]
-        return T.NB[:, a:1040 + 1024 * h:16]
+    def names_of(t, a, b):
+        return T.NB[:, 16 + 16 * a + cls[t]:16 + 16 * b:16]
 
     def mine(m, a, n):
         return T["LD%d" % m][:, rank, a:a + n]
+
+    def key(m, r):
+        return "M%d" % m if r == rank else "LD%d_%d" % (m, r)
 
     def self_out(t):
         n, vt, qt = "QX%d" % t, VTs[t], "QT%d" % t
@@ -191,20 +194,29 @@ def rank_program(g, core, T, topo):
 
     def repeat_names(t):
         qt = "QT%d" % t
-        ts(T.TQ[:, :], T[qt][:, 0:128], 2048.0, A.is_equal, qt, "TQ", 2048.0, A.mult)
-        tt(T.QC[:, 0:128], T.TQ[:, :], T[qt][:, 0:128], A.add, "TQ " + qt, "QC")
-        act(T.QR[:, :], T.QC[:, 0:128].indirect(T.IOW[:, :]), "QC IOW", "QR")
+
+        def copies():
+            for k in range(16):
+                act(T.QR[:, k:2048:16], T.QC[:, 0:128], "QC CM CV", "+QR", func=IDN, bias=T.CV[:, k:k + 1], scale=T.CM[:, k:k + 1])
+        return [lambda: ts(T.TQ[:, :], T[qt][:, 0:128], 2048.0, A.is_equal, qt, "TQ", 2048.0, A.mult),
+                lambda: tt(T.QC[:, 0:128], T.TQ[:, :], T[qt][:, 0:128], A.add, "TQ " + qt, "QC"), copies]
 
     def gather_sizes(q, lst, a, b):
         f = cp if q == "v" else act
-        f(T.XV[:, 16 * a:16 * b], T.XS[:, 0:2080].indirect(T[lst][:, a:b]), "XS XSp " + lst + ("_0" if b <= 64 else "_1"), "XV%d" % a)
+        f(T.XV[:, 16 * a:16 * b], T.XS[:, 0:2080].indirect(T[lst[:-2]][:, a:b]), "XS XSp " + lst, "XV%d" % a)
 
-    def degrees(h, keys, mx):
-        o = T.P2[:, 64 * h:64 * h + 64]
+    def degrees(a, b, keys, mx):
+        o = T.P2[:, a:b]
         if mx:
-            mm(o, T.IDB[:, :], T.MX[:, 1024 * h + 15:1024 * h + 1024:16], True, False, "IDB MX", "P2")
+            mm(o, T.IDB[:, :], T.MX[:, 16 * a + 15:16 * b:16], True, False, "IDB MX", "P2")
         for k in range(16):
-            mm(o, T.IDB[:, :], T.XV[:, 1024 * h + k:1024 * h + 1024:16], k == 0 and not mx, k == 15, "IDB " + keys, "P2")
+            mm(o, T.IDB[:, :], T.XV[:, 16 * a + k:16 * b:16], k == 0 and not mx, k == 15, "IDB " + keys, "P2")
+
+    gaps = {}
+
+    def gap(t, at):
+        for f in gaps.get((t, at), ()):
+            f()
 
     def select(t):
         ts(T.HR[:, :], T.P2[:, 0:128], T.LIMA[:, 0:1], A.is_le, "P2 LIMA", "HR")
@@ -218,14 +230,18 @@ def rank_program(g, core, T, topo):
             tt(T.HT[:, :], T.P3[:, 0:128], T.THR[:, :], A.is_ge, "P3 THR", "HT")
         for b in range(2):
             mm(T.P4[:, 128 * b:128 * b + 128], T.TRI[:, :], T.HT[:, :], True, True, "TRI HT", "P4")
+        gap(t, "rank")
         tt(T.CMP[:, :], T.P4[:, 0:256], T.SB[:, :], A.is_le, "P4 SB", "CMP")
         for b in range(2):
             mm(T.P5[:, 2 * b:2 * b + 2], T.CMP[:, 128 * b:128 * b + 128], T.WTS[:, :], True, True, "CMP WTS", "P5")
+        gap(t, "lanes")
         cp(T.LW[:, :], T.P5[:, 0:4:2], "P5", "LW")
+
+    ahead = [0, 1, 5]
 
     def places(t):
         for b in range(2):
-            ts(mine(t, VOFF + b, 1), T.P5[:, 2 * b + 1:2 * b + 2], float(cls[t] + 16), A.add, "P5 COL", "+M%d" % t, TRV[b], A.min)
+            ts(mine(ahead[t], VOFF + b, 1), T.P5[:, 2 * b + 1:2 * b + 2], float(cls[t] + 16), A.add, "P5 COL", "+M%d" % ahead[t], TRV[b], A.min)
 
     def at_pivots(buf):
         return T[buf][:, 0:136].indirect(T.LW[:, :])
@@ -251,15 +267,14 @@ def rank_program(g, core, T, topo):
                 wr["LD%d_%d" % (m, r)] = [("r", "a%d_%d" % (m, r), len(ne) if T.cores[r] in near else len(fe), {})]
 
     def unpack(m, buf, a, n):
-        keys = " ".join("M%d" % m if r == rank else "LD%d_%d" % (m, r) for r in range(8))
-        cp(T["%s%d" % (buf, m)][:, :], T["LD%d" % m][:, :, a:a + n], keys, "%s%d" % (buf, m))
+        cp(T["%s%d" % (buf, m)][:, :], T["LD%d" % m][:, :, a:a + n], " ".join(key(m, r) for r in range(8)), "%s%d" % (buf, m))
 
-    def pivots(tab, m, val, keys):
-        cp(T[tab][:, 0:W].indirect(T["OF%d" % m][:, :]), T["%s%d" % (val, m)][:, :], "OF%d %s%d" % (m, val, m), keys)
+    def pivots(tab, m, val, keys, o=None):
+        o = m if o is None else o
+        cp(TAB[tab].indirect(T["OF%d" % o][:, :]), T["%s%d" % (val, m)][:, :], "OF%d %s%d" % (o, val, m), keys)
 
-    def winners(tab, m, val, vm):
-        for r in range(7, -1, -1):
-            cp(T[tab][:, 0:W].indirect(T["OE%d" % m][:, 2 * r:2 * r + 2]), T["%s%d" % (val, vm)][:, 32 * r:32 * r + 32], "OE%d %s%d" % (m, val, vm), tab)
+    def new_j(m, n, r):
+        cp(TAB["JT"].indirect(T["OE%d" % m][:, n * r + n - 2:n * r + n]), T["LD%d" % m][:, r, VREP:VREP + 32], "OE%d %s" % (m, key(m, r)), "JT")
 
     def update(m):
         unpack(m, "OF", VOFF, 2)
@@ -270,25 +285,30 @@ def rank_program(g, core, T, topo):
 
     def count():
         ts(T.PR[:, :], T.P5[:, 0:4:2], 127.5, A.is_le, "P5", "PR")
-        mm(T.P2[:, 0:2], T.ONEB[:, :], T.PR[:, :], True, True, "ONEB PR", "P2")
-        red(T.AF[:, :], T.P2[:, 0:2], A.add, "P2", "AF")
-        cp(T.AI[:, :], T.AF[:, :], "AF", "AI")
+        for b in range(2):
+            mm(T.P2[:, 0:1], T.ONEB[:, :], T.PR[:, b:b + 1], b == 0, b == 1, "ONEB PR", "P2")
+        cp(T.AI[:, :], T.P2[:, 0:1], "P2", "AI")
         ts(T.AM[:, :], T.AI[:, :], 7, A.bitwise_and, "AI", "AM")
         tt(T.LIMA[:, :], T.AM[:, :], T.LIMI[:, :], A.add, "AM LIMI", "LIMA")
 
     def empty_covered(t):
         for h in range(2):
             ts(T.UN[:, 64 * h:64 * h + 64], T["P%d" % h][:, 0:64], 0.0, A.is_lt, "P%d" % h, "+UN", 2048.0, A.mult)
-        for h in range(2):
-            tt(names_of(t, h), T.UN[:, 64 * h:64 * h + 64], names_of(t, h), A.max, "UN NB%d" % h, "NB%d" % h)
+        tt(names_of(t, 0, 128), T.UN[:, :], names_of(t, 0, 128), A.max, "UN " + NBK, NBK)
+
+    def claim_keys():
+        mm(T.P6[:, :], T.BO32[:, :], T.X2[:, :], False, True, "BO32 X2", "P6")
+
+    def best_key():
+        scan(T.KS[:, :], T.RST[:, :], T.P6[:, :], 0.0, A.mult, A.max, "RST P6", "KS")
 
     def lanes_to_pivots(t):
         qt, oq = "QT%d" % t, "OQ%d" % t
         for h in range(2):
-            act(T.XG[:, 1024 * h:1024 * h + 1024], T.XE[:, 0:2080].indirect(T[oq][:, 64 * h:64 * h + 64]), "XE " + oq, "XG%d" % h)
+            act(T.XG[:, 1024 * h:1024 * h + 1024], XEW.indirect(T[oq][:, 64 * h:64 * h + 64]), "XE " + oq, "XG%d" % h)
 
-        def cover(a, b, key):
-            tt(T.EQ[:, 16 * a:16 * b], T.NE[:, 0:2080].indirect(T[oq][:, a:b]), T.QR[:, 16 * a:16 * b], A.is_equal, "NE QR " + oq, key)
+        def cover(a, b, k):
+            tt(T.EQ[:, 16 * a:16 * b], NEW.indirect(T[oq][:, a:b]), T.QR[:, 16 * a:16 * b], A.is_equal, "NE QR " + oq, k)
         cover(0, 64, "EQ0")
         cover(64, 96, "EQ1")
         for h in range(2):
@@ -296,48 +316,54 @@ def rank_program(g, core, T, topo):
             mm(o, T.IDF[:, :], T[qt][:, 64 * h:64 * h + 64], True, False, "IDF " + qt, "P%d" % h)
             mm(o, T.IDB[:, :], T.KB[:, 0:64], False, False, "IDB KB", "P%d" % h)
         for h in range(2):
-            pb, s = "P%d" % h, 1024 * h
-            o = T[pb][:, 0:64]
             if h:
                 ts(T.UL[:, 0:64], T.P0[:, 0:64], 16.0, A.add, "P0", "UL_0", 2064.0, A.min)
                 cover(96, 128, "EQ2")
             for k in range(16):
-                mm(o, T.SA[:, 128 * k:128 * k + 128], T.XG[:, s + k:s + 1024:16], False, False, "SA XG%d" % h, pb)
-            for k in range(16):
-                mm(o, T.NI[:, :], T.EQ[:, s + k:s + 1024:16], False, k == 15, "NI " + ("EQ1 EQ2" if h else "EQ0"), pb)
-        gather_sizes("a", "UL", 0, 64)
+                mm(T["P%d" % h][:, 0:64], T.SA[:, 128 * k:128 * k + 128], T.EQ[:, 1024 * h + k:1024 * h + 1024:16], False, k == 15,
+                   "SA " + ("EQ1 EQ2" if h else "EQ0"), "P%d" % h)
+        gather_sizes("a", "UL_0", 0, 64)
         scan(T.MX[:, :], T.RSM[:, :], T.XG[:, :], 0.0, A.min, A.max, "RSM XG0 XG1", "MX")
         ts(T.UL[:, 64:128], T.P1[:, 0:64], 16.0, A.add, "P1", "UL_1", 2064.0, A.min)
-        gather_sizes("a", "UL", 64, 96)
-        gather_sizes("v", "UL", 96, 128)
+        gather_sizes("a", "UL_1", 64, 96)
+        gather_sizes("v", "UL_1", 96, 128)
         empty_covered(t)
-        degrees(0, "XV0", True)
-        degrees(1, "XV64 XV96", True)
+        gap(t, "degrees")
+        degrees(0, 64, "XV0", True)
+        degrees(64, 128, "XV64 XV96", True)
         for h in range(2):
             act(T.UA[:, 64 * h:64 * h + 64], T["P%d" % h][:, 0:64], "P%d" % h, "+UA", func=ActivationFunctionType.Abs)
         mm(T.P6[:, :], T.IDB[:, :], T.KC[:, :], True, False, "IDB KC", "P6")
         select(t)
         ts(T.EP[:, :], at_pivots(qt), 16.0, A.add, "%s %sp LW" % (qt, qt), "EP")
-        act(T.Q2[:, :], T.NE[:, 0:2080].indirect(T.EP[:, :]), "NE EP", "Q2")
-        act(T.X2[:, :], T.XE[:, 0:2080].indirect(T.EP[:, :]), "XE EP", "X2")
+        act(T.Q2[:, :], NEW.indirect(T.EP[:, :]), "NE EP", "Q2")
+        act(T.X2[:, :], XEW.indirect(T.EP[:, :]), "XE EP", "X2")
         cp(T.L16[:, :], at_pivots("LT"), "LT LW", "L16")
-        cp(mine(t, SIZES, 32), at_pivots("SZ"), "SZ SZp LW", "+M%d" % t)
+        cp(mine(ahead[t], SIZES, 32), at_pivots("SZ"), "SZ SZp LW", "+M%d" % ahead[t])
+        places(t)
+        if t == 2:
+            send(5)
         ts(T.QM[:, :], at_pivots(qt), -4080.0, A.add, "%s %sp LW" % (qt, qt), "QM")
         cp(T.OP[:, :], at_pivots("OWN"), "OWN OWNp LW", "OP")
-        places(t)
+        m = 4 if t == 1 else 3
+        ts(mine(m, VREP, 32), at_pivots(VTs[t]), 16.0, A.add, VTs[t] + " LW", "+M%d" % m)
 
     def new_names(t):
         vt = VTs[t]
+        if t == 1:
+            claim_keys()
         tt(T.MM[:, :], T[vt][:, 0:136].indirect(T.L16[:, :]), T.Q2[:, :], A.is_equal, vt + " L16 Q2", "MM")
         mm(T.P7[:, :], T.I4[:, :], T.MM[:, :], True, True, "I4 MM", "P7")
+        gap(t, "names")
         tt(T.CC[:, :], T.Q2[:, :], T.P7[:, :], A.add, "Q2 P7", "CC")
         scan(T.NS[:, :], T.RSTB[:, :], T.CC[:, :], 8192.0, A.add, A.min, "RSTB CC", "NS")
         tt(T.NM[:, :], T.NS[:, 15:512:16], T.OP[:, :], A.min, "NS OP", "NM")
         ts(mine(t, NAMES, 32), T.NM[:, :], 2048.0, A.min, "NM", "+M%d" % t)
 
     def win_row(t):
-        mm(T.P6[:, :], T.BO32[:, :], T.X2[:, :], False, True, "BO32 X2", "P6")
-        scan(T.KS[:, :], T.RST[:, :], T.P6[:, :], 0.0, A.mult, A.max, "RST P6", "KS")
+        if t == 2:
+            claim_keys()
+            best_key()
         cp(T.KI[:, :], T.KS[:, 15:512:16], "KS", "KI")
         ts(T.K5[:, :], T.KI[:, :], 31, A.bitwise_and, "KI", "K5")
         ts(T.OH[:, :], T.K5[:, :], CODE, A.is_equal, "K5 COL", "OH")
@@ -360,15 +386,17 @@ def rank_program(g, core, T, topo):
         scan(T.DX[:, :], T.R32[:, :], T.ED[:, :], 0.0, A.mult, A.max, "R32 ED", "DX")
         for b in range(2):
             ts(mine(m, EOFF + b, 1), T.DX[:, 32 * b + 31:32 * b + 32], col[b], A.max, "DX COL " + tl, "+M%d" % m, TRE[b], A.min)
+        if m == 4:
+            ts(mine(m, EOFF2, 2), mine(m, EOFF, 2), float(W), A.add, "M4", "+M4")
 
-    for h in range(2):
-        nk, s = "NB%d" % h, slice(64 * h, 64 * h + 64)
-        ts(T.OQ0[:, s], names_of(0, h), 16.0, A.add, nk, "OQ0_%d" % h)
-        gather_sizes("a", "OQ0", 64 * h, 64 * h + 32)
-        gather_sizes("v", "OQ0", 64 * h + 32, 64 * h + 64)
-        degrees(h, "XV%d XV%d" % (64 * h, 64 * h + 32), False)
-        cp(T.QT0[:, s], names_of(0, h), nk, "+QT0")
-    act(T.XE[:, :], T.NE[:, :], "NE", "XE", func=IDN, bias=-1.0, scale=0.0)
+    for j, (a, b) in enumerate(((0, 64), (64, 96), (96, 128))):
+        c = (a + b) // 2
+        ts(T.OQ0[:, a:b], names_of(0, a, b), 16.0, A.add, "NB%d" % j, "OQ0_%d" % j)
+        gather_sizes("a", "OQ0_%d" % j, a, c)
+        gather_sizes("v", "OQ0_%d" % j, c, b)
+        degrees(a, b, "XV%d XV%d" % (a, c), False)
+        cp(T.QT0[:, a:b], names_of(0, a, b), "NB%d" % j, "+QT0")
+    act(T.NX[:, W:2 * W], T.NX[:, 0:W], "NE", "XE", func=IDN, bias=-1.0, scale=0.0)
     for k in range(16):
         act(T.SA[:, 128 * k:128 * k + 128], T.IDB[:, :], "IDB CA", "+SA", scale=T.CA[:, k:k + 1])
     self_out(0)
@@ -379,9 +407,9 @@ def rank_program(g, core, T, topo):
     places(0)
     send(0)
 
-    for h in range(2):
-        cp(T.QT1[:, 64 * h:64 * h + 64], names_of(1, h), "NB%d" % h, "+QT1")
-    repeat_names(1)
+    cp(T.QT1[:, 0:128], names_of(1, 0, 128), NBK, "QT1")
+    for f in repeat_names(1):
+        f()
     ts(T.OQ1[:, :], T.QT1[:, 0:128], 16.0, A.add, "QT1", "OQ1")
     count()
     ts(T.PV[:, :], T.P4[:, 0:128], 32.0, A.is_le, "P4", "PV")
@@ -398,31 +426,33 @@ def rank_program(g, core, T, topo):
     iota(T.JT[:, 2064:2072], [[0, 8]], 4096, 0, "+JT")
 
     update(0)
+    more = repeat_names(2)
+    gaps[1, "rank"], gaps[1, "lanes"], gaps[1, "names"] = more[:1], more[1:2], [best_key, more[2]]
     lanes_to_pivots(1)
     new_names(1)
     send(1)
-    ts(mine(4, VREP, 32), at_pivots("VT1"), 16.0, A.add, "VT1 LW", "+M4")
     win_row(1)
     as_list("P3", T.P3[:, 0:32], "TM", "TL")
     claims(4, T.P4, "P4", "TL")
     send(4)
-    repeat_names(2)
     for k in range(16):
         act(T.SAF[:, 128 * k:128 * k + 128], T.IDF[:, :], "IDF CB", "+SAF", scale=T.CB[:, k:k + 1])
     count()
-    pivots("NB", 0, "NV", "NB0 NB1")
+    pivots("NB", 0, "NV", NBK)
+    pivots("XS", 0, "SV", "XS")
 
     update(1)
-    unpack(4, "OE", EOFF, 2)
-    winners("XE", 4, "SV", 1)
-    winners("NE", 4, "NV", 1)
+    unpack(4, "OE", EOFF2, 4)
+    for r in range(7, -1, -1):
+        cp(T.NX[:, 0:2 * W].indirect(T.OE4[:, 4 * r:4 * r + 4]), T.LD1[:, r, SIZES:SIZES + 64], "OE4 " + key(1, r), "NE XE")
+    todo = [lambda r=r: new_j(4, 4, r) for r in range(7, -1, -1)]
+    gaps[2, "degrees"], gaps[2, "rank"], gaps[2, "lanes"], gaps[2, "names"] = todo[:1], todo[1:2], todo[2:3], todo[3:6]
     lanes_to_pivots(2)
     new_names(2)
     send(2)
-    ts(mine(3, VREP, 32), at_pivots("VT0"), 16.0, A.add, "VT0 LW", "+M3")
     win_row(2)
-    unpack(4, "VR", VREP, 32)
-    winners("JT", 4, "VR", 4)
+    for f in todo[6:]:
+        f()
     for k in range(16):
         mm(T.P5[:, 0:128], T.SAF[:, 128 * k:128 * k + 128], T.JT[:, 16 + k:2064:16], k == 0, k == 15, "SAF JT", "P5")
     as_list("P3", T.P3[:, 0:32], "TM", "TL")
@@ -434,19 +464,19 @@ def rank_program(g, core, T, topo):
     claims(3, T.EM, "EM", "TL2")
     send(3)
 
-    pivots("NB", 1, "NV", "NB0 NB1")
-    unpack(2, "OF", VOFF, 2)
-    unpack(2, "NV", NAMES, 32)
-    pivots("NB", 2, "NV", "NB0 NB1")
-    dma("s", T.yn[:, :], T.NB[:, 16:2064], "o_n", "NB0 NB1", "")
-    unpack(2, "SV", SIZES, 32)
-    for m in range(3):
-        pivots("XS", m, "SV", "XS")
+    pivots("XS", 1, "SV", "XS")
+    unpack(5, "OF", VOFF, 2)
+    unpack(5, "SV", SIZES, 32)
+    pivots("XS", 5, "SV", "XS")
     dma("s", T.yx[:, :], T.XS[:, 16:2064], "o_x", "XS", "")
+    pivots("NB", 1, "NV", NBK)
+    unpack(2, "NV", NAMES, 32)
+    pivots("NB", 2, "NV", NBK, 5)
+    dma("s", T.yn[:, :], T.NB[:, 16:2064], "o_n", NBK, "")
     cp(T.JL[:, :], T.P5[:, 0:128], "P5", "JL")
     unpack(3, "OE", EOFF, 2)
-    unpack(3, "VR", VREP, 32)
-    winners("JT", 3, "VR", 3)
+    for r in range(7, -1, -1):
+        new_j(3, 2, r)
     act(T.YJ[:, 0:1024], T.JT[:, 0:2072].indirect(T.JL[:, 0:64]), "JT JL", "YJ0", func=IDN, bias=-16.0)
     ts(T.YJ[:, 1024:2048], T.JT[:, 0:2072].indirect(T.JL[:, 64:128]), -16.0, A.add, "JT JL", "YJ1")
     dma("a", T.yj[:, 0:1024], T.YJ[0:128:16, 0:1024], "o_j0", "YJ0", "")
@@ -454,7 +484,7 @@ def rank_program(g, core, T, topo):
 
     for q in ("v", "t", "a", "g"):
         g.wait_ge(T.sem["e" + q], cnt[q])
-    for s in ("d_x", "d_n0", "d_n1", "d_l", "o_n", "o_x", "o_j0", "o_j1"):
+    for s in ("d_x", "d_n0", "d_n1", "d_n2", "d_l", "o_n", "o_x", "o_j0", "o_j1"):
         g.wait_ge(T.sem[s], 16)
-    for m in range(5):
+    for m in range(6):
         g.wait_ge(T.sem["l%d" % m], nloc[m])

from concourse.bass import DstId, RemoteDMATransfer
from concourse.mybir import AluOpType, AxisListType, ActivationFunctionType

W = 2368
F, B, I, U = "float32", "bfloat16", "int32", "uint16"
SCRATCH = {}
for _names, _w, _d in (
        ("NX", 2 * W, F), ("NB JT", W, F), ("XS", W, B), ("SA EQ XG XV MX RSM", 2048, B), ("SAF QR YJ", 2048, F),
        ("RSTB Q2 KS CC NS", 512, F), ("KC X2 MM RST", 512, B), ("ONEB IDB I4 BO BO32 TRI HR HT PV PVB", 128, B), ("CMP", 256, B),
        ("IDF BOF TQ UA UN THR DQ", 128, F), ("SB", 256, F), ("WTS PR", 2, B), ("KB MB", 64, B), ("K4", 32, B),
        ("PI PA LIMI AI AM", 1, I), ("PF LIMA", 1, F), ("COL", 8, F), ("CA CB CM CV IO16", 16, F),
        ("LT VT0 VT1 QT0 QT1 QT2 QX0 QX1 QX2 QC OWN SZ", 136, F), ("OQ0 OQ1 OQ2 UL JL", 128, U),
        ("IO32 D2 QM OP NM OH PD TM TM2 TL TL2 JE", 32, F), ("IO64 MF ED EM DX R32", 64, F), ("LW UW", 2, U), ("EP L16", 32, U), ("KI K5", 32, I),
        ("NV0 NV1 NV2 SV0 SV1 SV5", 256, U), ("OF0 OF1 OF5 OE3", 16, U), ("OE4", 32, U)):
    for _n in _names.split():
        SCRATCH[_n] = ("sbuf", [128, _w], _d)
for _b in range(6):
    SCRATCH["LD%d" % _b] = ("sbuf", [128, 8, 104], U)
for _b in range(8):
    SCRATCH["P%d" % _b] = ("psum", [128, 512], F)
SEMAPHORES = ["ev", "et", "ea", "eg", "d_x", "d_n0", "d_n1", "d_n2", "d_l", "o_n", "o_x", "o_j0", "o_j1"]
SEMAPHORES += ["a%d_%d" % (m, r) for m in range(6) for r in range(8)] + ["l%d" % m for m in range(6)]
VOFF, SIZES, NAMES, EOFF2, EOFF, VREP = 0, 2, 34, 66, 68, 70
SPAN = [(0, 66), (0, 66), (34, 66), (68, 102), (66, 102), (0, 34)]


def rank_program(g, core, T, topo):
    rank = T.rank_of(core)
    if rank is None:
        return
    A = AluOpType
    IDN = ActivationFunctionType.Identity
    Q = {"v": g.vector, "t": g.tensor, "a": g.scalar, "g": g, "s": g.sync}
    cnt, wr, rd, nloc = {}, {}, {}, {}
    known = {q: {} for q in Q}

    def bank(k):
        return k[0] == "P" and k[1:].isdigit()

    def pre(q, R, Wk):
        evs = []
        for k in R:
            evs += wr.get(k, [])
            if bank(k):
                evs += [e for e in rd.get(k, []) if e[0] != q]
        for k in Wk:
            part = q == "t" or k[0] == "+"
            k = k.lstrip("+")
            evs += [e for e in wr.get(k, []) if not part or e[0] != q] + rd.get(k, [])
        top = {}
        for e in evs:
            top[e[1]] = max(top.get(e[1], 0), e[2])
        for e in sorted(evs, key=lambda e: -len(e[3])):
            if top[e[1]] == e[2] and known[q].get(e[1], 0) < e[2]:
                Q[q].wait_ge(T.sem[e[1]], e[2])
                for s, n in e[3].items():
                    known[q][s] = max(known[q].get(s, 0), n)
                known[q][e[1]] = e[2]

    def post(q, by, sem, n, R, Wk):
        ck = dict(known[by])
        ck[sem] = n
        ev = (q, sem, n, ck)
        Wk = [k.lstrip("+") for k in Wk]
        for k in Wk:
            wr[k] = [ev]
            rd[k] = []
        for k in R:
            if k not in Wk:
                rd[k] = [e for e in rd.get(k, []) if e[0] != q] + [ev]

    def op(q, f, R, Wk):
        R, Wk = R.split(), Wk.split()
        pre(q, R, Wk)
        cnt[q] = cnt.get(q, 0) + 1
        f().then_inc(T.sem["e" + q], 1)
        post(q, q, "e" + q, cnt[q], R, Wk)

    def dma(q, out, in_, sem, R, Wk):
        R, Wk = R.split(), Wk.split()
        pre(q, R, Wk)
        Q[q].dma_start(out, in_).then_inc(T.sem[sem], 16)
        post(sem, q, sem, 16, R, Wk)

    V = g.vector

    def cp(out, in_, R, Wk):
        op("v", lambda: V.tensor_copy(out=out, in_=in_), R, Wk)

    def ts(out, in0, s1, o0, R, Wk, s2=None, o1=None):
        if o1 is None:
            op("v", lambda: V.tensor_scalar(out=out, in0=in0, scalar1=s1, scalar2=None, op0=o0), R, Wk)
        else:
            op("v", lambda: V.tensor_scalar(out=out, in0=in0, scalar1=s1, scalar2=s2, op0=o0, op1=o1), R, Wk)

    def tt(out, in0, in1, o, R, Wk):
        op("v", lambda: V.tensor_tensor(out=out, in0=in0, in1=in1, op=o), R, Wk)

    def scan(out, d0, d1, init, o0, o1, R, Wk):
        op("v", lambda: V.tensor_tensor_scan(out=out, data0=d0, data1=d1, initial=init, op0=o0, op1=o1), R, Wk)

    def fill(ap, c, Wk):
        op("v", lambda: V.memset(ap, c), "", Wk)

    def mm(out, l, r, start, stop, R, Wk):
        op("t", lambda: g.tensor.matmul(out=out, lhsT=l, rhs=r, start=start, stop=stop), R, Wk)

    def act(out, in_, R, Wk, func=ActivationFunctionType.Copy, bias=0.0, scale=1.0):
        op("a", lambda: g.scalar.activation(out=out, in_=in_, func=func, bias=bias, scale=scale), R, Wk)

    def iota(out, pat, base, cm, Wk):
        op("g", lambda: g.iota(out, pat, base, cm, allow_small_or_imprecise_dtypes=True), "", Wk)

    def asel(out, in_, pat, o, fl, base, cm, R, Wk):
        op("g", lambda: g.affine_select(out, in_, pat, o, fl, base, cm), R, Wk)

    cls = [rank, 8 + rank, rank]
    VTs = ["VT0", "VT1", "VT0"]
    NBK = "NB0 NB1 NB2"
    TAB = {"NB": T.NB[:, 0:W], "XS": T.XS[:, 0:W], "NE": T.NX[:, 0:W], "XE": T.NX[:, W:2 * W], "JT": T.JT[:, 0:W]}
    NEW, XEW = T.NX[:, 0:2080], T.NX[:, W:W + 2080]

    dma("s", T.NB[:, 16:1040], T.nb[:, 0:1024], "d_n0", "", "NB0")
    dma("a", T.XS[:, 16:2064], T.xs[:, :], "d_x", "", "XS")
    dma("s", T.NB[:, 1040:1552], T.nb[:, 1024:1536], "d_n1", "", "NB1")
    dma("s", T.NB[:, 1552:2064], T.nb[:, 1536:2048], "d_n2", "", "NB2")
    dma("s", T.LIMI[:, :], T.lim[:, :], "d_l", "", "LIMI")

    fill(T.ONEB[:, :], 1.0, "ONEB")
    fill(T.WTS[:, 0:1], 1.0, "+WTS")
    fill(T.WTS[:, 1:2], 16.0, "+WTS")
    fill(T.XS[:, 0:16], 0.0, "+XSp")
    fill(T.XS[:, 2064:W], 0.0, "+XSp")
    asel(T.IDB[:, :], T.ONEB[:, :], [[-1, 128]], A.is_equal, 0.0, 0, 1, "ONEB", "IDB")
    asel(T.BO[:, :], T.ONEB[:, :], [[-16, 8], [0, 16]], A.is_ge, 0.0, 0, 1, "ONEB", "BO")
    asel(T.BO[:, :], T.BO[:, :], [[16, 8], [0, 16]], A.is_ge, 0.0, 15, -1, "BO", "BO")
    asel(T.TRI[:, :], T.ONEB[:, :], [[1, 128]], A.is_ge, 0.0, 0, -1, "ONEB", "TRI")
    asel(T.WTS[:, 1:2], T.WTS[:, 1:2], [[0, 1]], A.not_equal, 384.0, -127, 1, "WTS", "WTS")
    op("g", lambda: g.iota(T.PI[:, :], [[0, 1]], 0, 1), "", "PI")
    iota(T.VT0[:, :], [[16, 136]], cls[0], 0, "VT0")
    iota(T.SB[:, :], [[16, 2], [0, 8], [1, 16]], 0, 0, "SB")
    iota(T.IO16[:, :], [[1, 16]], 0, 0, "IO16")
    iota(T.IO32[:, :], [[0, 2], [1, 16]], 0, 0, "IO32")
    iota(T.IO64[:, :], [[-16, 2], [1, 32]], 0, 0, "IO64")
    iota(T.LT[:, :], [[1, 136]], 0, 0, "LT")
    iota(T.VT1[:, :], [[16, 136]], cls[1], 0, "VT1")
    iota(T.KC[:, :], [[0, 32], [-1, 16]], 31, 0, "KC")
    iota(T.NX[:, 0:W], [[0, W]], 2050, 0, "NE")
    for n in ("QT0", "QT1", "QT2"):
        fill(T[n][:, 128:136], 2048.0, n + "p")
    for n in ("QX0", "OWN"):
        fill(T[n][:, 128:136], 4096.0, n + "p")
    fill(T.SZ[:, 128:136], 0.0, "SZp")
    fill(T.KB[:, :], 131072.0, "KB")
    fill(T.K4[:, :], 4096.0, "K4")
    fill(T.RST[:, :], 1.0, "RST")
    fill(T.RST[:, 0:512:16], 0.0, "RST")
    fill(T.R32[:, :], 1.0, "R32")
    fill(T.R32[:, 0:64:32], 0.0, "R32")
    fill(T.RSTB[:, :], 0.0, "RSTB")
    fill(T.RSTB[:, 0:512:16], 8192.0, "RSTB")
    ts(T.PA[:, :], T.PI[:, :], 15, A.bitwise_and, "PI", "PA")
    cp(T.PF[:, :], T.PA[:, :], "PA", "PF")
    ts(T.COL[:, 0:1], T.PF[:, :], -1.0, A.mult, "PF", "+COL", 31.0, A.add)
    for j, b in enumerate((2080 + 32 * rank, 2096 + 32 * rank, 2336, 2352)):
        ts(T.COL[:, j + 1:j + 2], T.PF[:, :], float(b), A.add, "PF", "+COL")
    CODE, TRV, TRE = T.COL[:, 0:1], [T.COL[:, 1:2], T.COL[:, 2:3]], [T.COL[:, 3:4], T.COL[:, 4:5]]
    ts(T.CB[:, :], T.IO16[:, :], T.PF[:, 0:1], A.is_equal, "IO16 PF", "CB")
    ts(T.CM[:, :], T.IO16[:, :], T.PF[:, 0:1], A.not_equal, "IO16 PF", "CM")
    ts(T.CV[:, :], T.CB[:, :], 2050.0, A.mult, "CB", "CV")
    ts(T.CA[:, :], T.CB[:, :], -126976.0, A.mult, "CB", "CA", -4096.0, A.add)
    cp(T.IDF[:, :], T.IDB[:, :], "IDB", "IDF")
    ts(T.BO32[:, :], T.BO[:, :], 32.0, A.mult, "BO", "BO32")
    ts(T.I4[:, :], T.IDB[:, :], 4096.0, A.mult, "IDB", "I4")
    ts(T.D2[:, :], T.IO32[:, :], T.PF[:, 0:1], A.is_equal, "IO32 PF", "D2")
    ts(T.MF[:, :], T.IO64[:, :], T.PF[:, 0:1], A.is_ge, "IO64 PF", "MF", 8192.0, A.mult)
    ts(T.MB[:, :], T.MF[:, :], 4096.0, A.add, "MF", "MB")
    cp(T.BOF[:, :], T.BO[:, :], "BO", "BOF")

    def names_of(t, a, b):
        return T.NB[:, 16 + 16 * a + cls[t]:16 + 16 * b:16]

    def mine(m, a, n):
        return T["LD%d" % m][:, rank, a:a + n]

    def key(m, r):
        return "M%d" % m if r == rank else "LD%d_%d" % (m, r)

    def self_out(t):
        n, vt, qt = "QX%d" % t, VTs[t], "QT%d" % t
        tt(T.TQ[:, :], T[qt][:, 0:128], T[vt][:, 0:128], A.is_equal, qt + " " + vt, "TQ")
        ts(T.TQ[:, :], T.TQ[:, :], 4096.0, A.mult, "TQ", "TQ")
        tt(T[n][:, 0:128], T.TQ[:, :], T[qt][:, 0:128], A.max, "TQ " + qt, n)

    def repeat_names(t):
        qt = "QT%d" % t

        def copies():
            for k in range(16):
                act(T.QR[:, k:2048:16], T.QC[:, 0:128], "QC CM CV", "+QR", func=IDN, bias=T.CV[:, k:k + 1], scale=T.CM[:, k:k + 1])
        return [lambda: ts(T.TQ[:, :], T[qt][:, 0:128], 2048.0, A.is_equal, qt, "TQ", 2048.0, A.mult),
                lambda: tt(T.QC[:, 0:128], T.TQ[:, :], T[qt][:, 0:128], A.add, "TQ " + qt, "QC"), copies]

    def gather_sizes(q, lst, a, b):
        f = cp if q == "v" else act
        f(T.XV[:, 16 * a:16 * b], T.XS[:, 0:2080].indirect(T[lst[:-2]][:, a:b]), "XS XSp " + lst, "XV%d" % a)

    def degrees(a, b, keys, mx):
        o = T.P2[:, a:b]
        if mx:
            mm(o, T.IDB[:, :], T.MX[:, 16 * a + 15:16 * b:16], True, False, "IDB MX", "P2")
        for k in range(16):
            mm(o, T.IDB[:, :], T.XV[:, 16 * a + k:16 * b:16], k == 0 and not mx, k == 15, "IDB " + keys, "P2")

    gaps = {}

    def gap(t, at):
        for f in gaps.get((t, at), ()):
            f()

    def select(t):
        ts(T.HR[:, :], T.P2[:, 0:128], T.LIMA[:, 0:1], A.is_le, "P2 LIMA", "HR")
        mm(T.P3[:, 0:128], T.HR[:, :], T.BO[:, :], True, True, "HR BO", "P3")
        ts(T.SZ[:, 0:128], T.P2[:, 0:128], 255.0, A.min, "P2", "SZ")
        if t:
            tt(T.OWN[:, 0:128], T.UA[:, :], T["QX%d" % t][:, 0:128], A.max, "UA QX%d" % t, "OWN")
        if t < 2:
            ts(T.HT[:, :], T.P3[:, 0:128], 9.0, A.is_ge, "P3", "HT")
        else:
            tt(T.HT[:, :], T.P3[:, 0:128], T.THR[:, :], A.is_ge, "P3 THR", "HT")
        for b in range(2):
            mm(T.P4[:, 128 * b:128 * b + 128], T.TRI[:, :], T.HT[:, :], True, True, "TRI HT", "P4")
        gap(t, "rank")
        tt(T.CMP[:, :], T.P4[:, 0:256], T.SB[:, :], A.is_le, "P4 SB", "CMP")
        for b in range(2):
            mm(T.P5[:, 2 * b:2 * b + 2], T.CMP[:, 128 * b:128 * b + 128], T.WTS[:, :], True, True, "CMP WTS", "P5")
        gap(t, "lanes")
        cp(T.LW[:, :], T.P5[:, 0:4:2], "P5", "LW")

    ahead = [0, 1, 5]

    def places(t):
        for b in range(2):
            ts(mine(ahead[t], VOFF + b, 1), T.P5[:, 2 * b + 1:2 * b + 2], float(cls[t] + 16), A.add, "P5 COL", "+M%d" % ahead[t], TRV[b], A.min)

    def at_pivots(buf):
        return T[buf][:, 0:136].indirect(T.LW[:, :])

    near = [c for c in T.cores if topo.chip(c) == topo.chip(core) and c != core]
    far = [c for c in T.cores if topo.chip(c) != topo.chip(core)]
    fe = topo.engines(core, far[0])
    ne = [e for e in topo.engines(core, near[0]) if e not in fe][:2]

    def send(m):
        a, b = SPAN[m]
        tr = []
        for cs, es in ((far, fe), (near, ne)):
            ids = [DstId(rid=topo.addr(c)[0], pnc=topo.addr(c)[1]) for c in cs]
            tr.append(RemoteDMATransfer(dst_ids=ids, dma_engine_mask=sum(1 << e for e in es), remote_sem=T.sem["a%d_%d" % (m, rank)],
                                        srcs=[mine(m, a, b - a)], dsts=[mine(m, a, b - a)] * len(cs)))
        pre("g", ["M%d" % m], [])
        g.remote_dma_fused(tr, local_sem=T.sem["l%d" % m])
        nloc[m] = len(fe) + len(ne)
        post("l%d" % m, "g", "l%d" % m, nloc[m], ["M%d" % m], [])
        for r in range(8):
            if r != rank:
                wr["LD%d_%d" % (m, r)] = [("r", "a%d_%d" % (m, r), len(ne) if T.cores[r] in near else len(fe), {})]

    def unpack(m, buf, a, n):
        cp(T["%s%d" % (buf, m)][:, :], T["LD%d" % m][:, :, a:a + n], " ".join(key(m, r) for r in range(8)), "%s%d" % (buf, m))

    def pivots(tab, m, val, keys, o=None):
        o = m if o is None else o
        cp(TAB[tab].indirect(T["OF%d" % o][:, :]), T["%s%d" % (val, m)][:, :], "OF%d %s%d" % (o, val, m), keys)

    def new_j(m, n, r):
        cp(TAB["JT"].indirect(T["OE%d" % m][:, n * r + n - 2:n * r + n]), T["LD%d" % m][:, r, VREP:VREP + 32], "OE%d %s" % (m, key(m, r)), "JT")

    def update(m):
        unpack(m, "OF", VOFF, 2)
        unpack(m, "SV", SIZES, 32)
        pivots("XE", m, "SV", "XE")
        unpack(m, "NV", NAMES, 32)
        pivots("NE", m, "NV", "NE")

    def count():
        ts(T.PR[:, :], T.P5[:, 0:4:2], 127.5, A.is_le, "P5", "PR")
        for b in range(2):
            mm(T.P2[:, 0:1], T.ONEB[:, :], T.PR[:, b:b + 1], b == 0, b == 1, "ONEB PR", "P2")
        cp(T.AI[:, :], T.P2[:, 0:1], "P2", "AI")
        ts(T.AM[:, :], T.AI[:, :], 7, A.bitwise_and, "AI", "AM")
        tt(T.LIMA[:, :], T.AM[:, :], T.LIMI[:, :], A.add, "AM LIMI", "LIMA")

    def empty_covered(t):
        for h in range(2):
            ts(T.UN[:, 64 * h:64 * h + 64], T["P%d" % h][:, 0:64], 0.0, A.is_lt, "P%d" % h, "+UN", 2048.0, A.mult)
        tt(names_of(t, 0, 128), T.UN[:, :], names_of(t, 0, 128), A.max, "UN " + NBK, NBK)

    def claim_keys():
        mm(T.P6[:, :], T.BO32[:, :], T.X2[:, :], False, True, "BO32 X2", "P6")

    def best_key():
        scan(T.KS[:, :], T.RST[:, :], T.P6[:, :], 0.0, A.mult, A.max, "RST P6", "KS")

    def lanes_to_pivots(t):
        qt, oq = "QT%d" % t, "OQ%d" % t
        for h in range(2):
            act(T.XG[:, 1024 * h:1024 * h + 1024], XEW.indirect(T[oq][:, 64 * h:64 * h + 64]), "XE " + oq, "XG%d" % h)

        def cover(a, b, k):
            tt(T.EQ[:, 16 * a:16 * b], NEW.indirect(T[oq][:, a:b]), T.QR[:, 16 * a:16 * b], A.is_equal, "NE QR " + oq, k)
        cover(0, 64, "EQ0")
        cover(64, 96, "EQ1")
        for h in range(2):
            o = T["P%d" % h][:, 0:64]
            mm(o, T.IDF[:, :], T[qt][:, 64 * h:64 * h + 64], True, False, "IDF " + qt, "P%d" % h)
            mm(o, T.IDB[:, :], T.KB[:, 0:64], False, False, "IDB KB", "P%d" % h)
        for h in range(2):
            if h:
                ts(T.UL[:, 0:64], T.P0[:, 0:64], 16.0, A.add, "P0", "UL_0", 2064.0, A.min)
                cover(96, 128, "EQ2")
            for k in range(16):
                mm(T["P%d" % h][:, 0:64], T.SA[:, 128 * k:128 * k + 128], T.EQ[:, 1024 * h + k:1024 * h + 1024:16], False, k == 15,
                   "SA " + ("EQ1 EQ2" if h else "EQ0"), "P%d" % h)
        gather_sizes("a", "UL_0", 0, 64)
        scan(T.MX[:, :], T.RSM[:, :], T.XG[:, :], 0.0, A.min, A.max, "RSM XG0 XG1", "MX")
        ts(T.UL[:, 64:128], T.P1[:, 0:64], 16.0, A.add, "P1", "UL_1", 2064.0, A.min)
        gather_sizes("a", "UL_1", 64, 96)
        gather_sizes("v", "UL_1", 96, 128)
        empty_covered(t)
        gap(t, "degrees")
        degrees(0, 64, "XV0", True)
        degrees(64, 128, "XV64 XV96", True)
        for h in range(2):
            act(T.UA[:, 64 * h:64 * h + 64], T["P%d" % h][:, 0:64], "P%d" % h, "+UA", func=ActivationFunctionType.Abs)
        mm(T.P6[:, :], T.IDB[:, :], T.KC[:, :], True, False, "IDB KC", "P6")
        select(t)
        ts(T.EP[:, :], at_pivots(qt), 16.0, A.add, "%s %sp LW" % (qt, qt), "EP")
        act(T.Q2[:, :], NEW.indirect(T.EP[:, :]), "NE EP", "Q2")
        act(T.X2[:, :], XEW.indirect(T.EP[:, :]), "XE EP", "X2")
        cp(T.L16[:, :], at_pivots("LT"), "LT LW", "L16")
        cp(mine(ahead[t], SIZES, 32), at_pivots("SZ"), "SZ SZp LW", "+M%d" % ahead[t])
        places(t)
        if t == 2:
            send(5)
        ts(T.QM[:, :], at_pivots(qt), -4080.0, A.add, "%s %sp LW" % (qt, qt), "QM")
        cp(T.OP[:, :], at_pivots("OWN"), "OWN OWNp LW", "OP")
        m = 4 if t == 1 else 3
        ts(mine(m, VREP, 32), at_pivots(VTs[t]), 16.0, A.add, VTs[t] + " LW", "+M%d" % m)

    def new_names(t):
        vt = VTs[t]
        if t == 1:
            claim_keys()
        tt(T.MM[:, :], T[vt][:, 0:136].indirect(T.L16[:, :]), T.Q2[:, :], A.is_equal, vt + " L16 Q2", "MM")
        mm(T.P7[:, :], T.I4[:, :], T.MM[:, :], True, True, "I4 MM", "P7")
        gap(t, "names")
        tt(T.CC[:, :], T.Q2[:, :], T.P7[:, :], A.add, "Q2 P7", "CC")
        scan(T.NS[:, :], T.RSTB[:, :], T.CC[:, :], 8192.0, A.add, A.min, "RSTB CC", "NS")
        tt(T.NM[:, :], T.NS[:, 15:512:16], T.OP[:, :], A.min, "NS OP", "NM")
        ts(mine(t, NAMES, 32), T.NM[:, :], 2048.0, A.min, "NM", "+M%d" % t)

    def win_row(t):
        if t == 2:
            claim_keys()
            best_key()
        cp(T.KI[:, :], T.KS[:, 15:512:16], "KS", "KI")
        ts(T.K5[:, :], T.KI[:, :], 31, A.bitwise_and, "KI", "K5")
        ts(T.OH[:, :], T.K5[:, :], CODE, A.is_equal, "K5 COL", "OH")
        tt(T.PD[:, :], T.OH[:, :], T.QM[:, :], A.mult, "OH QM", "PD")
        mm(T.P3[:, 0:32], T.IDB[:, :], T.K4[:, :], True, False, "IDB K4", "P3")
        mm(T.P3[:, 0:32], T.BOF[:, :], T.PD[:, :], False, True, "BOF PD", "P3")
        for b in range(2 if t == 1 else 0):
            o = T.P4[:, 32 * b:32 * b + 32]
            mm(o, T.IDB[:, :], T.MB[:, 32 * b:32 * b + 32], True, False, "IDB MB", "P4")
            mm(o, T.BOF[:, :], T.PD[:, :], False, True, "BOF PD", "P4")

    def as_list(rk, rep, tm, tl):
        tt(T[tm][:, :], rep, T.D2[:, :], A.mult, rk + " D2", tm)
        scan(T[tl][:, :], T.RST[:, 0:32], T[tm][:, :], 0.0, A.mult, A.add, "RST " + tm, tl)

    def claims(m, em, ek, tl):
        col = [T[tl][:, 15:16], T[tl][:, 31:32]]
        for b in range(2):
            ts(T.ED[:, 32 * b:32 * b + 32], em[:, 32 * b:32 * b + 32], col[b], A.is_equal, ek + " " + tl, "+ED", 4096.0, A.mult)
        scan(T.DX[:, :], T.R32[:, :], T.ED[:, :], 0.0, A.mult, A.max, "R32 ED", "DX")
        for b in range(2):
            ts(mine(m, EOFF + b, 1), T.DX[:, 32 * b + 31:32 * b + 32], col[b], A.max, "DX COL " + tl, "+M%d" % m, TRE[b], A.min)
        if m == 4:
            ts(mine(m, EOFF2, 2), mine(m, EOFF, 2), float(W), A.add, "M4", "+M4")

    for j, (a, b) in enumerate(((0, 64), (64, 96), (96, 128))):
        c = (a + b) // 2
        ts(T.OQ0[:, a:b], names_of(0, a, b), 16.0, A.add, "NB%d" % j, "OQ0_%d" % j)
        gather_sizes("a", "OQ0_%d" % j, a, c)
        gather_sizes("v", "OQ0_%d" % j, c, b)
        degrees(a, b, "XV%d XV%d" % (a, c), False)
        cp(T.QT0[:, a:b], names_of(0, a, b), "NB%d" % j, "+QT0")
    act(T.NX[:, W:2 * W], T.NX[:, 0:W], "NE", "XE", func=IDN, bias=-1.0, scale=0.0)
    for k in range(16):
        act(T.SA[:, 128 * k:128 * k + 128], T.IDB[:, :], "IDB CA", "+SA", scale=T.CA[:, k:k + 1])
    self_out(0)
    cp(T.LIMA[:, :], T.LIMI[:, :], "LIMI", "LIMA")
    select(0)
    ts(mine(0, NAMES, 32), at_pivots("QX0"), 2048.0, A.min, "QX0 QX0p LW", "+M0")
    cp(mine(0, SIZES, 32), at_pivots("SZ"), "SZ SZp LW", "+M0")
    places(0)
    send(0)

    cp(T.QT1[:, 0:128], names_of(1, 0, 128), NBK, "QT1")
    for f in repeat_names(1):
        f()
    ts(T.OQ1[:, :], T.QT1[:, 0:128], 16.0, A.add, "QT1", "OQ1")
    count()
    ts(T.PV[:, :], T.P4[:, 0:128], 32.0, A.is_le, "P4", "PV")
    tt(T.PVB[:, :], T.PV[:, :], T.HT[:, :], A.mult, "PV HT", "PVB")
    mm(T.P7[:, 0:128], T.PVB[:, :], T.IDB[:, :], True, True, "PVB IDB", "P7")
    ts(T.THR[:, :], T.PVB[:, :], 100.0, A.mult, "PVB", "THR", 9.0, A.add)
    self_out(1)
    ts(T.DQ[:, :], T.P7[:, 0:128], 2048.0, A.mult, "P7", "DQ")
    tt(T.QT2[:, 0:128], T.DQ[:, :], T.QT0[:, 0:128], A.max, "DQ QT0", "QT2")
    ts(T.OQ2[:, :], T.QT2[:, 0:128], 16.0, A.add, "QT2", "OQ2")
    self_out(2)
    iota(T.RSM[:, :], [[0, 128], [256, 16]], 0, 0, "RSM")
    iota(T.JT[:, 0:2064], [[1, 2064]], 0, 0, "JT")
    iota(T.JT[:, 2064:2072], [[0, 8]], 4096, 0, "+JT")

    update(0)
    more = repeat_names(2)
    gaps[1, "rank"], gaps[1, "lanes"], gaps[1, "names"] = more[:1], more[1:2], [best_key, more[2]]
    lanes_to_pivots(1)
    new_names(1)
    send(1)
    win_row(1)
    as_list("P3", T.P3[:, 0:32], "TM", "TL")
    claims(4, T.P4, "P4", "TL")
    send(4)
    for k in range(16):
        act(T.SAF[:, 128 * k:128 * k + 128], T.IDF[:, :], "IDF CB", "+SAF", scale=T.CB[:, k:k + 1])
    count()
    pivots("NB", 0, "NV", NBK)
    pivots("XS", 0, "SV", "XS")

    update(1)
    unpack(4, "OE", EOFF2, 4)
    for r in range(7, -1, -1):
        cp(T.NX[:, 0:2 * W].indirect(T.OE4[:, 4 * r:4 * r + 4]), T.LD1[:, r, SIZES:SIZES + 64], "OE4 " + key(1, r), "NE XE")
    todo = [lambda r=r: new_j(4, 4, r) for r in range(7, -1, -1)]
    gaps[2, "degrees"], gaps[2, "rank"], gaps[2, "lanes"], gaps[2, "names"] = todo[:1], todo[1:2], todo[2:3], todo[3:6]
    lanes_to_pivots(2)
    new_names(2)
    send(2)
    win_row(2)
    for f in todo[6:]:
        f()
    for k in range(16):
        mm(T.P5[:, 0:128], T.SAF[:, 128 * k:128 * k + 128], T.JT[:, 16 + k:2064:16], k == 0, k == 15, "SAF JT", "P5")
    as_list("P3", T.P3[:, 0:32], "TM", "TL")
    ts(T.UW[:, :], T.TL[:, 15:32:16], 2064.0, A.min, "TL", "UW")
    cp(T.JE[:, :], T.JT[:, 0:2072].indirect(T.UW[:, :]), "JT UW", "JE")
    as_list("JE", T.JE[:, :], "TM2", "TL2")
    for b in range(2):
        tt(T.EM[:, 32 * b:32 * b + 32], T.JE[:, :], T.MF[:, 32 * b:32 * b + 32], A.add, "JE MF", "+EM")
    claims(3, T.EM, "EM", "TL2")
    send(3)

    pivots("XS", 1, "SV", "XS")
    unpack(5, "OF", VOFF, 2)
    unpack(5, "SV", SIZES, 32)
    pivots("XS", 5, "SV", "XS")
    dma("s", T.yx[:, :], T.XS[:, 16:2064], "o_x", "XS", "")
    pivots("NB", 1, "NV", NBK)
    unpack(2, "NV", NAMES, 32)
    pivots("NB", 2, "NV", NBK, 5)
    dma("s", T.yn[:, :], T.NB[:, 16:2064], "o_n", NBK, "")
    cp(T.JL[:, :], T.P5[:, 0:128], "P5", "JL")
    unpack(3, "OE", EOFF, 2)
    for r in range(7, -1, -1):
        new_j(3, 2, r)
    act(T.YJ[:, 0:1024], T.JT[:, 0:2072].indirect(T.JL[:, 0:64]), "JT JL", "YJ0", func=IDN, bias=-16.0)
    ts(T.YJ[:, 1024:2048], T.JT[:, 0:2072].indirect(T.JL[:, 64:128]), -16.0, A.add, "JT JL", "YJ1")
    dma("a", T.yj[:, 0:1024], T.YJ[0:128:16, 0:1024], "o_j0", "YJ0", "")
    dma("s", T.yj[:, 1024:2048], T.YJ[0:128:16, 1024:2048], "o_j1", "YJ1", "")

    for q in ("v", "t", "a", "g"):
        g.wait_ge(T.sem["e" + q], cnt[q])
    for s in ("d_x", "d_n0", "d_n1", "d_n2", "d_l", "o_n", "o_x", "o_j0", "o_j1"):
        g.wait_ge(T.sem[s], 16)
    for m in range(6):
        g.wait_ge(T.sem["l%d" % m], nloc[m])
